import numpy as np
import ml_dtypes


def mxq(x, axis, fmt="e4m3"):
    dtype, down = {"e4m3": (ml_dtypes.float8_e4m3fn, 7), "e5m2": (ml_dtypes.float8_e5m2, 14)}[fmt]
    v = np.moveaxis(np.asarray(x, np.float32).astype(ml_dtypes.bfloat16).astype(np.float64), axis, -1)
    blocks = v.reshape(v.shape[:-1] + (-1, 32))
    amax = np.abs(blocks).max(-1, keepdims=True)
    byte = np.maximum(np.where(amax > 0, np.frexp(amax)[1] - 1 + 127, 0) - down, 1)
    scale = np.exp2(byte - 127.0)
    codes = (blocks / scale).astype(np.float32).astype(dtype).astype(np.float64)
    return np.moveaxis((codes * scale).reshape(v.shape), -1, axis)


WIDE = False


def mx_kscale(k):
    if not WIDE:
        return np.ones(k)
    levels = np.array([10, -10, 5, -5, 0])
    if k % 512:
        return np.exp2(np.random.permutation(np.resize(levels, k // 32))).repeat(32)
    a = np.empty((k // 512, 16))
    for p in range(k // 512):
        a[p, :8] = np.random.permutation(np.resize(levels, 8))
        for g in range(8):
            far = levels[np.abs(levels - a[p, g]) >= 10]
            a[p, g + 8] = far[np.random.randint(len(far))]
    return np.exp2(a.ravel()).repeat(32)


def f64(x):
    return np.asarray(x).astype(np.float64)


def striped(idx):
    return np.tile(np.asarray(idx).reshape(-1, 16).T, (8, 1)).astype(np.uint16)


def unstriped(offs):
    return offs[:16].T.reshape(-1).astype(np.int64)


E2M1 = np.array([0.0, 0.5, 1.0, 1.5, 2.0, 3.0, 4.0, 6.0, -0.0, -0.5, -1.0, -1.5, -2.0, -3.0, -4.0, -6.0])


def pack_weight(w, fmt):
    k, n = w.shape
    w = f64(np.asarray(w, np.float32).astype(ml_dtypes.bfloat16)).reshape(k // 32, 32, n)
    amax = np.abs(w).max(1)
    if fmt == "e4m3":
        byte = np.frexp(amax)[1] - 1 + 127 - 7
    else:
        mant, ex = np.frexp(amax / 6.0)
        byte = np.where(mant > 0.5, ex, ex - 1) + 127
    byte = np.clip(np.where(amax > 0, byte, 1), 1, 254)
    scaled = (w * np.exp2(127.0 - byte)[:, None, :]).reshape(k, n).astype(np.float32)
    by_word = np.ascontiguousarray(scaled.reshape(k // 512, 128, 4, n).transpose(0, 1, 3, 2))
    if fmt == "e4m3":
        words = by_word.astype(ml_dtypes.float8_e4m3fn).view(np.uint8)
    else:
        c = by_word.astype(ml_dtypes.float4_e2m1fn).view(np.uint8) & 0xF
        words = (c[..., 0::2] | (c[..., 1::2] << 4)).reshape(k // 512, 128, 2 * n)
    return np.ascontiguousarray(words), np.ascontiguousarray(byte.astype(np.uint8).reshape(k // 512, 16, n))


def unpack_weight(words, scales, fmt):
    g, _, n = scales.shape
    words = np.ascontiguousarray(words).reshape(g, 128, n, -1)
    if fmt == "e4m3":
        vals = words.view(ml_dtypes.float8_e4m3fn).astype(np.float64)
    else:
        nib = np.empty((g, 128, n, 4), np.uint8)
        nib[..., 0::2] = words & 0xF
        nib[..., 1::2] = words >> 4
        vals = E2M1[nib]
    vals = vals * np.repeat(np.exp2(scales.astype(np.float64) - 127.0), 8, axis=1)[..., None]
    return vals.transpose(0, 1, 3, 2).reshape(g * 512, n)


def bf(x):
    return np.asarray(x, np.float32).astype(ml_dtypes.bfloat16)


def planes(Y):
    r, m = Y.shape
    b = f64(bf(Y)).reshape(r // 32, 32, m)
    amax = np.abs(b).max(1)
    byte = np.clip(np.where(amax > 0, np.frexp(amax)[1] - 1 + 127 - 7, 1), 1, 254)
    codes = (b * np.exp2(127.0 - byte)[:, None, :]).reshape(r, m).astype(np.float32).astype(ml_dtypes.float8_e4m3fn).view(np.uint8)
    words = codes.reshape(r // 512, 128, 4, m).transpose(0, 1, 3, 2)
    return np.ascontiguousarray(words), np.ascontiguousarray(byte.astype(np.uint8).reshape(r // 512, 16, m))


D, T, I, Q, E = 512, 2048, 512, 256, 512


def setup_inputs():
    n = np.random.standard_normal
    idx = np.random.permutation(T)[:I]
    fd = mx_kscale(D)
    fi = mx_kscale(I)
    ti = np.ones(T)
    ti[idx] = fi
    keysp = pack_weight(n((D, T)) / fd[:, None], "e2m1")
    return {
        "query": (n((D, Q)) * 0.2 / np.sqrt(D) * fd[:, None]).astype(np.float32),
        "keys_words": keysp[0],
        "keys_scales": keysp[1],
        "kn": np.tile(np.random.uniform(1.5, 2.5, T), (128, 1)).astype(np.float32),
        "qn": (np.random.uniform(1.5, 2.5, (Q, 1))).astype(np.float32),
        "size": (np.random.uniform(0.5, 2.0, (1, I)) * fi).astype(np.float32),
        "vals": (n((E, T)) / ti).astype(np.float32),
        "offs": striped(idx),
    }


def reference(query, keys_words, keys_scales, kn, qn, size, vals, offs):
    idx = unstriped(offs)
    keysu = unpack_weight(keys_words, keys_scales, "e2m1")
    queryq = mxq(f64(query), 0, "e4m3")
    keysidxg = keysu[:, idx]
    a = queryq.T @ keysidxg
    r = 1.0 / (f64(qn) + f64(kn)[:1][:, idx] - 2.0 * a + 0.1)
    w = r * f64(size) / np.sum(r, axis=1, keepdims=True)
    wt = w.T
    vt = f64(vals)[:, idx].T
    vtq = mxq(vt, 0, "e4m3")
    wtq = mxq(wt, 0, "e4m3")
    o = vtq.T @ wtq
    words, scales = planes(o)
    return o, words, scales

@@ -1,0 +1,250 @@
+from contextlib import ExitStack
+
+import concourse.mybir as mybir
+from concourse.masks import make_identity
+
+D, T, I, Q, E = 512, 2048, 512, 256, 512
+FLOPS = 2 * D * Q * I + 2 * I * E * Q
+
+F32 = mybir.dt.float32
+BF16 = mybir.dt.bfloat16
+I32 = mybir.dt.int32
+U32 = mybir.dt.uint32
+U16 = mybir.dt.uint16
+U8 = mybir.dt.uint8
+FP8X4 = mybir.dt.float8_e4m3fn_x4
+FP4X4 = mybir.dt.float4_e2m1fn_x4
+ACT = mybir.ActivationFunctionType
+ALU = mybir.AluOpType
+
+P = 128
+PACK = 4
+BANK = 512
+HALVES = Q // P
+
+
+def tile_attend_necread_pl_kernel(
+    tc, query, keys_words, keys_scales, kn, qn, size, vals, offs, out_0, out_1, out_2
+):
+    nc = tc.nc
+    with ExitStack() as ctx:
+        keep = ctx.enter_context(tc.tile_pool(name="keep", bufs=1))
+        stage = ctx.enter_context(tc.tile_pool(name="stage", bufs=1))
+        psum = ctx.enter_context(tc.psum_pool(name="psum", bufs=1))
+
+        def sb(name, shape, dtype, tag=None):
+            return keep.tile(shape, dtype, name=name, tag=tag or name, align_bytes=64)
+
+        def landing(name, shape, dtype, place):
+            return stage.tile(shape, dtype, name=name, tag=f"landing{place}", align_bytes=64)
+
+        def bank(name, tag):
+            return psum.tile([P, BANK], F32, name=name, tag=tag)
+
+        offsets = keep.tile([P, I // 16], U16, name="offsets")
+        nc.sync.dma_start(offsets[:], offs)
+
+        warm = sb("warm", [P, 1], F32)
+        warm_out = sb("warm_out", [P, 1], F32)
+        nc.vector.memset(warm[:], 1.0)
+        nc.scalar.activation(warm_out[:], warm[:], ACT.Abs_reciprocal_sqrt)
+
+        qn_raw = landing("qn_raw", [P, HALVES], F32, 0)
+        kn_win = landing("kn_win", [P, T], F32, 1)
+        key_word_win = landing("key_word_win", [P, T], U16, 2)
+        key_scale_win = landing("key_scale_win", [P, T], U8, 3)
+        nc.gpsimd.memset(key_scale_win[:].bitcast(U32), 0)
+        nc.vector.memset(kn_win[0 : P - 1, :], 0.0)
+        ident = sb("ident", [P, P], F32)
+        make_identity(nc, ident[:])
+
+        with nc.allow_non_contiguous_dma(reason="one number a query row"):
+            nc.sync.dma_start(qn_raw[:], qn.rearrange("(j p) o -> p (j o)", p=P))
+        nc.sync.dma_start(kn_win[P - 1 : P, :], kn[0:1, :])
+        size_col = sb("size_col", [P, PACK], F32)
+        nc.sync.dma_start(size_col[:], size.rearrange("o (p t) -> p (o t)", t=PACK))
+        q_raw = sb("q_raw", [P, PACK, Q], F32)
+        nc.sync.dma_start(q_raw[:], query.rearrange("(p j) q -> p j q", j=PACK))
+        nc.sync.dma_start(key_word_win[:].bitcast(I32), keys_words[0].bitcast(I32))
+        for quad in range(4):
+            nc.sync.dma_start(
+                key_scale_win[32 * quad : 32 * quad + 4, :].bitcast(I32),
+                keys_scales[0, 4 * quad : 4 * quad + 4, :].bitcast(I32),
+            )
+        qn_col = sb("qn_col", [P, HALVES], F32)
+        nc.gpsimd.tensor_scalar_add(qn_col[:], qn_raw[:], 0.1)
+
+        q_grouped = sb("q_grouped", [P, Q, PACK], BF16)
+        nc.scalar.copy(
+            q_grouped[:].rearrange("p (c i) j -> p c j i", i=4),
+            q_raw[:].rearrange("p j (c i) -> p c j i", i=4),
+        )
+        q_codes = sb("q_codes", [P, Q], U32)
+        q_scales = sb("q_scales", [P, Q], U8)
+
+        def quantise_queries():
+            nc.vector.quantize_mx(
+                out=q_codes[:].bitcast(FP8X4),
+                scales=q_scales[:],
+                in_=q_grouped[:].rearrange("p q j -> p (q j)"),
+            )
+
+        kn_g = sb("kn_g", [P, I], F32)
+        nc.vector.tensor_copy(kn_g[:], kn_win[:].indirect(offsets[:]))
+        key_words, key_scales = [], []
+        for h in range(2):
+            picks = offsets[:, 16 * h : 16 * (h + 1)]
+            sc = sb(f"key_scales{h}", [P, I // 2], U8)
+            nc.vector.tensor_copy(sc[:], key_scale_win[:].indirect(picks))
+            wd = sb(f"key_words{h}", [P, I // 2], U16)
+            nc.vector.tensor_copy(wd[:], key_word_win[:].indirect(picks))
+            key_scales.append(sc)
+            key_words.append(wd)
+            if h == 0:
+                quantise_queries()
+
+        vals_rows = vals.rearrange("(p r) t -> r p t", r=PACK)
+        val_wins = []
+        for r in range(PACK):
+            win = landing(f"val_win{r}", [P, T], F32, r)
+            nc.sync.dma_start(win[:], vals_rows[r])
+            val_wins.append(win)
+
+        kn_ps = bank("kn_ps", "b4")
+        for c in range(4):
+            nc.tensor.transpose(kn_ps[:, c * P : (c + 1) * P], kn_g[:, c * P : (c + 1) * P], ident[:])
+        kn_col = sb("kn_col", [P, 4], F32)
+        nc.scalar.copy(kn_col[:], kn_ps[:, P - 1 : BANK : P])
+        size_ps = bank("size_ps", "b5")
+        for t in range(PACK):
+            nc.tensor.transpose(
+                size_ps[:, t * P : (t + 1) * P], size_col[:, t : t + 1].to_broadcast([P, P]), ident[:]
+            )
+
+        part = []
+        for h in range(2):
+            score_ps = bank(f"score_ps{h}", f"b{h}")
+            for c in (2 * h, 2 * h + 1):
+                nc.tensor.matmul_mx(
+                    out=score_ps[:, (c % 2) * Q : (c % 2 + 1) * Q],
+                    lhsT=key_words[h][:, (c % 2) * P : (c % 2 + 1) * P].bitcast(FP4X4),
+                    lhsT_scale=key_scales[h][:, (c % 2) * P : (c % 2 + 1) * P],
+                    rhs=q_codes[:].bitcast(FP8X4),
+                    rhs_scale=q_scales[:],
+                    start=True,
+                    stop=True,
+                )
+            for c in (2 * h, 2 * h + 1):
+                piece = sb(f"part{c}", [P, Q], F32)
+                nc.scalar.activation(
+                    piece[:], score_ps[:, (c % 2) * Q : (c % 2 + 1) * Q], ACT.Identity,
+                    bias=kn_col[:, c : c + 1], scale=-2.0,
+                )
+                part.append(piece)
+
+        dist_ps = []
+        for j in range(HALVES):
+            ps = bank(f"dist_ps{j}", f"b{2 + j}")
+            for c in range(4):
+                nc.tensor.transpose(ps[:, c * P : (c + 1) * P], part[c][:, j * P : (j + 1) * P], ident[:])
+            dist_ps.append(ps)
+
+        def gather_values(r):
+            g = sb(f"val_g{r}", [P, I], BF16)
+            nc.vector.tensor_copy(g[:], val_wins[r][:].indirect(offsets[:]))
+            return g
+
+        def turn_pairs(src, ps, grouped):
+            words = src.bitcast(F32)
+            for u in range(2):
+                nc.tensor.transpose(ps[:, u * P : (u + 1) * P], words[:, u : 2 * P : 2], ident[:])
+            nc.scalar.copy(
+                grouped.bitcast(F32).rearrange("p (c u) -> p c u", u=2),
+                ps[:, 0 : 2 * P].rearrange("p (u c) -> p c u", u=2),
+            )
+
+        def quantise(name, grouped, width):
+            codes = sb(f"{name}_codes", [P, width], U32)
+            scales = sb(f"{name}_scales", [P, width], U8)
+            nc.vector.quantize_mx(out=codes[:].bitcast(FP8X4), scales=scales[:], in_=grouped)
+            return codes, scales
+
+        def values_planes(rs):
+            grouped = sb(f"val_grouped{rs[0]}", [P, len(rs) * I], BF16)
+            for n, r in enumerate(rs):
+                turn_pairs(gather_values(r)[:], bank(f"val_ps{r}", f"b{6 + r % 2}"), grouped[:, n * I : (n + 1) * I])
+            codes, scales = quantise(f"val{rs[0]}", grouped[:], len(rs) * P)
+            return [(codes[:, n * P : (n + 1) * P], scales[:, n * P : (n + 1) * P]) for n in range(len(rs))]
+
+        w_grouped = sb("w_grouped", [P, Q * PACK], BF16)
+
+        def weights_half(j):
+            root = sb(f"root{j}", [P, I], F32)
+            nc.scalar.activation(root[:], dist_ps[j][:], ACT.Abs_reciprocal_sqrt, bias=qn_col[:, j : j + 1])
+            sgn = sb(f"sgn{j}", [P, I], F32)
+            nc.scalar.activation(sgn[:], dist_ps[j][:], ACT.Sign, bias=qn_col[:, j : j + 1])
+            mag = sb(f"mag{j}", [P, I], F32)
+            nc.scalar.activation(mag[:], root[:], ACT.Square)
+            recip = landing(f"recip{j}", [P, I], F32, 2 + j)
+            total = sb(f"total{j}", [P, 1], F32)
+            nc.vector.scalar_tensor_tensor(
+                recip[:], sgn[:], 1.0, mag[:], ALU.mult, ALU.mult, accum_out=total[:]
+            )
+            inv = sb(f"inv{j}", [P, 1], F32)
+            nc.vector.reciprocal(inv[:], total[:])
+            w = sb(f"w{j}", [P, I], BF16)
+            nc.vector.scalar_tensor_tensor(
+                w[:].rearrange("p (s t) -> p s t", t=PACK),
+                recip[:].rearrange("p (s t) -> p s t", t=PACK),
+                inv[:],
+                size_ps[:].rearrange("p (t s) -> p s t", t=PACK),
+                ALU.mult,
+                ALU.mult,
+            )
+            turn_pairs(w[:], bank(f"w_ps{j}", f"b{2 + j}"), w_grouped[:, j * I : (j + 1) * I])
+
+        vq = values_planes([0, 1]) + values_planes([2])
+        weights_half(0)
+        vq = vq + values_planes([3])
+        weights_half(1)
+        w_codes, w_scales = quantise("w", w_grouped[:], Q)
+
+        out_rows = out_0.rearrange("(p r) q -> p r q", r=PACK)
+        out_words = out_1[0].rearrange("p q r -> p (q r)").bitcast(I32)
+        y_scales = sb("y_scales", [P, Q], U8)
+        for j in range(HALVES):
+            cols = slice(j * P, (j + 1) * P)
+            ps = bank(f"y_ps{j}", f"b{j}")
+            for r in range(PACK):
+                nc.tensor.matmul_mx(
+                    out=ps[:, r * P : (r + 1) * P],
+                    lhsT=vq[r][0].bitcast(FP8X4),
+                    lhsT_scale=vq[r][1],
+                    rhs=w_codes[:, cols].bitcast(FP8X4),
+                    rhs_scale=w_scales[:, cols],
+                    start=True,
+                    stop=True,
+                )
+            y_grouped = sb(f"y_grouped{j}", [P, P, PACK], BF16)
+            y = sb(f"y{j}", [P, PACK, P], F32)
+            permuted = ps[:].rearrange("p (r q) -> p q r", r=PACK)
+            if j == 0:
+                nc.vector.tensor_copy(y_grouped[:], permuted)
+                nc.scalar.copy(y[:].rearrange("p r q -> p (r q)"), ps[:])
+            else:
+                nc.scalar.copy(y_grouped[:], permuted)
+                nc.vector.tensor_copy(y[:].rearrange("p r q -> p (r q)"), ps[:])
+            y_codes = sb(f"y_codes{j}", [P, P], U32)
+            nc.vector.quantize_mx(
+                out=y_codes[:].bitcast(FP8X4),
+                scales=y_scales[:, cols],
+                in_=y_grouped[:].rearrange("p q r -> p (q r)"),
+            )
+            nc.sync.dma_start(out_rows[:, :, cols], y[:])
+            nc.sync.dma_start(out_words[:, cols], y_codes[:].bitcast(I32))
+        for quad in range(4):
+            queue = nc.sync if quad % 2 == 0 else nc.scalar
+            queue.dma_start(
+                out_2[0, 4 * quad : 4 * quad + 4, :].bitcast(I32),
+                y_scales[32 * quad : 32 * quad + 4, :].bitcast(I32),
+            )

@@ -21,6 +21,8 @@ P = 128
 PACK = 4
 BANK = 512
 HALVES = Q // P
+QUADS = 4
+KN_SPLIT = 1280
 
 
 def tile_attend_necread_pl_kernel(
@@ -29,48 +31,48 @@ def tile_attend_necread_pl_kernel(
     nc = tc.nc
     with ExitStack() as ctx:
         keep = ctx.enter_context(tc.tile_pool(name="keep", bufs=1))
-        stage = ctx.enter_context(tc.tile_pool(name="stage", bufs=1))
         psum = ctx.enter_context(tc.psum_pool(name="psum", bufs=1))
 
-        def sb(name, shape, dtype, tag=None):
-            return keep.tile(shape, dtype, name=name, tag=tag or name, align_bytes=64)
+        def sb(name, shape, dtype, place=None):
+            return keep.tile(shape, dtype, name=name, tag=place or name, align_bytes=64)
 
-        def landing(name, shape, dtype, place):
-            return stage.tile(shape, dtype, name=name, tag=f"landing{place}", align_bytes=64)
+        def bank(name, number):
+            return psum.tile([P, BANK], F32, name=name, tag=f"bank{number}")
 
-        def bank(name, tag):
-            return psum.tile([P, BANK], F32, name=name, tag=tag)
+        def quantise(codes, scales, grouped):
+            nc.vector.quantize_mx(out=codes.bitcast(FP8X4), scales=scales, in_=grouped)
 
         offsets = keep.tile([P, I // 16], U16, name="offsets")
         nc.sync.dma_start(offsets[:], offs)
 
-        warm = sb("warm", [P, 1], F32)
-        warm_out = sb("warm_out", [P, 1], F32)
-        nc.vector.memset(warm[:], 1.0)
-        nc.scalar.activation(warm_out[:], warm[:], ACT.Abs_reciprocal_sqrt)
+        qn_raw = sb("qn_raw", [P, HALVES], F32, "place0")
+        kn_win = sb("kn_win", [P, T], F32, "place1")
+        q_raw = sb("q_raw", [P, PACK, Q], F32, "place2")
+        key_scale_win = sb("key_scale_win", [P, T], U8)
 
-        qn_raw = landing("qn_raw", [P, HALVES], F32, 0)
-        kn_win = landing("kn_win", [P, T], F32, 1)
-        key_word_win = landing("key_word_win", [P, T], U16, 2)
-        key_scale_win = landing("key_scale_win", [P, T], U8, 3)
         nc.gpsimd.memset(key_scale_win[:].bitcast(U32), 0)
-        nc.vector.memset(kn_win[0 : P - 1, :], 0.0)
         ident = sb("ident", [P, P], F32)
         make_identity(nc, ident[:])
+        warm = sb("warm", [P, 1], F32)
+        nc.vector.memset(warm[:], 1.0)
+        nc.vector.memset(kn_win[0 : P - 1, 0:KN_SPLIT], 0.0)
+        nc.gpsimd.memset(kn_win[0 : P - 1, KN_SPLIT:T], 0.0)
 
+        nc.sync.dma_start(kn_win[P - 1 : P, :], kn[0:1, :])
         with nc.allow_non_contiguous_dma(reason="one number a query row"):
             nc.sync.dma_start(qn_raw[:], qn.rearrange("(j p) o -> p (j o)", p=P))
-        nc.sync.dma_start(kn_win[P - 1 : P, :], kn[0:1, :])
         size_col = sb("size_col", [P, PACK], F32)
         nc.sync.dma_start(size_col[:], size.rearrange("o (p t) -> p (o t)", t=PACK))
-        q_raw = sb("q_raw", [P, PACK, Q], F32)
         nc.sync.dma_start(q_raw[:], query.rearrange("(p j) q -> p j q", j=PACK))
+        key_word_win = sb("key_word_win", [P, T], U16, "place3")
         nc.sync.dma_start(key_word_win[:].bitcast(I32), keys_words[0].bitcast(I32))
-        for quad in range(4):
+        for quad in range(QUADS):
             nc.sync.dma_start(
                 key_scale_win[32 * quad : 32 * quad + 4, :].bitcast(I32),
                 keys_scales[0, 4 * quad : 4 * quad + 4, :].bitcast(I32),
             )
+        warm_out = sb("warm_out", [P, 1], F32)
+        nc.scalar.activation(warm_out[:], warm[:], ACT.Abs_reciprocal_sqrt)
         qn_col = sb("qn_col", [P, HALVES], F32)
         nc.gpsimd.tensor_scalar_add(qn_col[:], qn_raw[:], 0.1)
 
@@ -79,171 +81,196 @@ def tile_attend_necread_pl_kernel(
             q_grouped[:].rearrange("p (c i) j -> p c j i", i=4),
             q_raw[:].rearrange("p j (c i) -> p c j i", i=4),
         )
-        q_codes = sb("q_codes", [P, Q], U32)
-        q_scales = sb("q_scales", [P, Q], U8)
-
-        def quantise_queries():
-            nc.vector.quantize_mx(
-                out=q_codes[:].bitcast(FP8X4),
-                scales=q_scales[:],
-                in_=q_grouped[:].rearrange("p q j -> p (q j)"),
-            )
 
         kn_g = sb("kn_g", [P, I], F32)
         nc.vector.tensor_copy(kn_g[:], kn_win[:].indirect(offsets[:]))
-        key_words, key_scales = [], []
+        key_words = sb("key_words", [P, I], U16)
+        nc.vector.tensor_copy(key_words[:], key_word_win[:].indirect(offsets[:]))
+        q_codes = sb("q_codes", [P, Q], U32)
+        q_scales = sb("q_scales", [P, Q], U8)
+        key_scales = sb("key_scales", [P, I], U8)
         for h in range(2):
-            picks = offsets[:, 16 * h : 16 * (h + 1)]
-            sc = sb(f"key_scales{h}", [P, I // 2], U8)
-            nc.vector.tensor_copy(sc[:], key_scale_win[:].indirect(picks))
-            wd = sb(f"key_words{h}", [P, I // 2], U16)
-            nc.vector.tensor_copy(wd[:], key_word_win[:].indirect(picks))
-            key_scales.append(sc)
-            key_words.append(wd)
+            nc.vector.tensor_copy(
+                key_scales[:, h * 2 * P : (h + 1) * 2 * P],
+                key_scale_win[:].indirect(offsets[:, 16 * h : 16 * (h + 1)]),
+            )
             if h == 0:
-                quantise_queries()
+                quantise(q_codes[:], q_scales[:], q_grouped[:].rearrange("p q j -> p (q j)"))
 
         vals_rows = vals.rearrange("(p r) t -> r p t", r=PACK)
         val_wins = []
         for r in range(PACK):
-            win = landing(f"val_win{r}", [P, T], F32, r)
+            win = sb(f"val_win{r}", [P, T], F32, f"place{r}")
             nc.sync.dma_start(win[:], vals_rows[r])
             val_wins.append(win)
 
-        kn_ps = bank("kn_ps", "b4")
+        kn_ps = bank("kn_ps", 4)
         for c in range(4):
             nc.tensor.transpose(kn_ps[:, c * P : (c + 1) * P], kn_g[:, c * P : (c + 1) * P], ident[:])
         kn_col = sb("kn_col", [P, 4], F32)
         nc.scalar.copy(kn_col[:], kn_ps[:, P - 1 : BANK : P])
-        size_ps = bank("size_ps", "b5")
+        kn_row_ps = bank("kn_row_ps", 5)
+        for c in range(4):
+            nc.tensor.transpose(
+                kn_row_ps[:, c * P : (c + 1) * P], kn_col[:, c : c + 1].to_broadcast([P, P]), ident[:]
+            )
+        lengths = sb("lengths", [P, I], F32, "lengths")
+        nc.scalar.activation(lengths[:], kn_row_ps[:], ACT.Identity, bias=qn_col[:, 0:1])
+        size_ps = bank("size_ps", 4)
+        size_dealt = size_ps[:].rearrange("p (u s e) -> p u e s", u=2, e=2)
         for t in range(PACK):
             nc.tensor.transpose(
-                size_ps[:, t * P : (t + 1) * P], size_col[:, t : t + 1].to_broadcast([P, P]), ident[:]
+                size_dealt[:, t // 2, t % 2, :], size_col[:, t : t + 1].to_broadcast([P, P]), ident[:]
             )
 
         part = []
         for h in range(2):
-            score_ps = bank(f"score_ps{h}", f"b{h}")
+            score_ps = bank(f"score_ps{h}", 1 + h)
             for c in (2 * h, 2 * h + 1):
                 nc.tensor.matmul_mx(
-                    out=score_ps[:, (c % 2) * Q : (c % 2 + 1) * Q],
-                    lhsT=key_words[h][:, (c % 2) * P : (c % 2 + 1) * P].bitcast(FP4X4),
-                    lhsT_scale=key_scales[h][:, (c % 2) * P : (c % 2 + 1) * P],
-                    rhs=q_codes[:].bitcast(FP8X4),
-                    rhs_scale=q_scales[:],
+                    out=score_ps[:, (c % 2) * P : (c % 2 + 1) * P],
+                    lhsT=key_words[:, c * P : (c + 1) * P].bitcast(FP4X4),
+                    lhsT_scale=key_scales[:, c * P : (c + 1) * P],
+                    rhs=q_codes[:, P:Q].bitcast(FP8X4),
+                    rhs_scale=q_scales[:, P:Q],
+                    start=True,
+                    stop=True,
+                )
+            if h == 1:
+                row_ps = bank("row_ps", 0)
+                nc.tensor.matmul_mx(
+                    out=row_ps[:],
+                    lhsT=q_codes[:, 0:P].bitcast(FP8X4),
+                    lhsT_scale=q_scales[:, 0:P],
+                    rhs=key_words[:].bitcast(FP4X4),
+                    rhs_scale=key_scales[:],
                     start=True,
                     stop=True,
                 )
             for c in (2 * h, 2 * h + 1):
-                piece = sb(f"part{c}", [P, Q], F32)
+                piece = sb(f"part{c}", [P, P], F32)
                 nc.scalar.activation(
-                    piece[:], score_ps[:, (c % 2) * Q : (c % 2 + 1) * Q], ACT.Identity,
+                    piece[:], score_ps[:, (c % 2) * P : (c % 2 + 1) * P], ACT.Identity,
                     bias=kn_col[:, c : c + 1], scale=-2.0,
                 )
                 part.append(piece)
 
-        dist_ps = []
-        for j in range(HALVES):
-            ps = bank(f"dist_ps{j}", f"b{2 + j}")
-            for c in range(4):
-                nc.tensor.transpose(ps[:, c * P : (c + 1) * P], part[c][:, j * P : (j + 1) * P], ident[:])
-            dist_ps.append(ps)
+        dist0 = sb("dist0", [P, I], F32)
+        nc.vector.scalar_tensor_tensor(dist0[:], row_ps[:], -2.0, lengths[:], ALU.mult, ALU.add)
+        dist1 = bank("dist1", 3)
+        for c in range(4):
+            nc.tensor.transpose(dist1[:, c * P : (c + 1) * P], part[c][:], ident[:])
 
-        def gather_values(r):
-            g = sb(f"val_g{r}", [P, I], BF16)
-            nc.vector.tensor_copy(g[:], val_wins[r][:].indirect(offsets[:]))
-            return g
-
-        def turn_pairs(src, ps, grouped):
-            words = src.bitcast(F32)
-            for u in range(2):
-                nc.tensor.transpose(ps[:, u * P : (u + 1) * P], words[:, u : 2 * P : 2], ident[:])
-            nc.scalar.copy(
-                grouped.bitcast(F32).rearrange("p (c u) -> p c u", u=2),
-                ps[:, 0 : 2 * P].rearrange("p (u c) -> p c u", u=2),
-            )
-
-        def quantise(name, grouped, width):
-            codes = sb(f"{name}_codes", [P, width], U32)
-            scales = sb(f"{name}_scales", [P, width], U8)
-            nc.vector.quantize_mx(out=codes[:].bitcast(FP8X4), scales=scales[:], in_=grouped)
-            return codes, scales
-
-        def values_planes(rs):
-            grouped = sb(f"val_grouped{rs[0]}", [P, len(rs) * I], BF16)
-            for n, r in enumerate(rs):
-                turn_pairs(gather_values(r)[:], bank(f"val_ps{r}", f"b{6 + r % 2}"), grouped[:, n * I : (n + 1) * I])
-            codes, scales = quantise(f"val{rs[0]}", grouped[:], len(rs) * P)
-            return [(codes[:, n * P : (n + 1) * P], scales[:, n * P : (n + 1) * P]) for n in range(len(rs))]
-
-        w_grouped = sb("w_grouped", [P, Q * PACK], BF16)
-
-        def weights_half(j):
-            root = sb(f"root{j}", [P, I], F32)
-            nc.scalar.activation(root[:], dist_ps[j][:], ACT.Abs_reciprocal_sqrt, bias=qn_col[:, j : j + 1])
-            sgn = sb(f"sgn{j}", [P, I], F32)
-            nc.scalar.activation(sgn[:], dist_ps[j][:], ACT.Sign, bias=qn_col[:, j : j + 1])
-            mag = sb(f"mag{j}", [P, I], F32)
+        mags, signs = [], []
+        for j, (dist, bias) in enumerate(((dist0, 0.0), (dist1, qn_col[:, 1:2]))):
+            dealt = dist[:].rearrange("p (s u e) -> p u s e", u=2, e=2)
+            root = sb(f"root{j}", [P, 2, P, 2], F32, f"root{j}")
+            nc.scalar.activation(root[:], dealt, ACT.Abs_reciprocal_sqrt, bias=bias)
+            sign = sb(f"sign{j}", [P, 2, P, 2], F32)
+            nc.scalar.activation(sign[:], dealt, ACT.Sign, bias=bias)
+            mag = sb(f"mag{j}", [P, 2, P, 2], F32)
             nc.scalar.activation(mag[:], root[:], ACT.Square)
-            recip = landing(f"recip{j}", [P, I], F32, 2 + j)
-            total = sb(f"total{j}", [P, 1], F32)
-            nc.vector.scalar_tensor_tensor(
-                recip[:], sgn[:], 1.0, mag[:], ALU.mult, ALU.mult, accum_out=total[:]
-            )
-            inv = sb(f"inv{j}", [P, 1], F32)
-            nc.vector.reciprocal(inv[:], total[:])
-            w = sb(f"w{j}", [P, I], BF16)
-            nc.vector.scalar_tensor_tensor(
-                w[:].rearrange("p (s t) -> p s t", t=PACK),
-                recip[:].rearrange("p (s t) -> p s t", t=PACK),
-                inv[:],
-                size_ps[:].rearrange("p (t s) -> p s t", t=PACK),
-                ALU.mult,
-                ALU.mult,
-            )
-            turn_pairs(w[:], bank(f"w_ps{j}", f"b{2 + j}"), w_grouped[:, j * I : (j + 1) * I])
+            mags.append(mag[:].rearrange("p u s e -> p (u s e)"))
+            signs.append(sign[:].rearrange("p u s e -> p (u s e)"))
 
-        vq = values_planes([0, 1]) + values_planes([2])
-        weights_half(0)
-        vq = vq + values_planes([3])
-        weights_half(1)
-        w_codes, w_scales = quantise("w", w_grouped[:], Q)
+        val_grouped = [sb("val_grouped0", [P, 2 * I], BF16, "root1"), sb("val_grouped1", [P, 2 * I], BF16, "root0")]
+        val_ps = [bank("val_ps0", 6), bank("val_ps1", 7)]
+
+        def values_plane(r):
+            picked = sb(f"val_picked{r}", [P, I], BF16, "lengths" if r == 0 else None)
+            nc.vector.tensor_copy(picked[:], val_wins[r][:].indirect(offsets[:]))
+            words = picked[:].bitcast(F32)
+            for u in range(2):
+                at = (2 * (r % 2) + u) * P
+                nc.tensor.transpose(val_ps[r // 2][:, at : at + P], words[:, u : 2 * P : 2], ident[:])
+            planes = {1: (0, 2), 2: (2, 3), 3: (3, 4)}.get(r)
+            if planes:
+                a, b = planes
+                held = val_ps[r // 2][:, (a % 2) * 2 * P : (a % 2 + b - a) * 2 * P]
+                nc.scalar.copy(
+                    val_grouped[r // 2][:, (a % 2) * I : (a % 2 + b - a) * I].bitcast(F32).rearrange("p (r c u) -> p r c u", c=P, u=2),
+                    held.rearrange("p (r u c) -> p r c u", c=P, u=2),
+                )
+
+        def reciprocals(j, recip):
+            total = sb(f"total{j}", [P, 1], F32)
+            nc.vector.scalar_tensor_tensor(recip, signs[j], 1.0, mags[j], ALU.mult, ALU.mult, accum_out=total[:])
+            return total
+
+        def weights(j, recip, inv, place):
+            w = sb(f"w{j}", [P, I], BF16, place)
+            nc.vector.scalar_tensor_tensor(w[:], recip, inv, size_ps[:], ALU.mult, ALU.mult)
+            words = w[:].bitcast(F32)
+            w_ps = bank(f"w_ps{j}", 3 + 2 * j)
+            for u in range(2):
+                nc.tensor.transpose(w_ps[:, u * P : (u + 1) * P], words[:, u * P : (u + 1) * P], ident[:])
+            grouped = sb(f"w_grouped{j}", [P, P * PACK], BF16)
+            nc.scalar.copy(
+                grouped[:].bitcast(F32).rearrange("p (c u) -> p c u", u=2),
+                w_ps[:, 0 : 2 * P].rearrange("p (u c) -> p c u", u=2),
+            )
+            return grouped
+
+        values_plane(0)
+        values_plane(1)
+        recip0 = sb("recip0", [P, I], F32, "place1")
+        total0 = reciprocals(0, recip0[:])
+        values_plane(2)
+        shared = sb("shared", [P, I + 8], F32, "place2")
+        inv0, recip1 = shared[:, I : I + 1], shared[:, 0:I]
+        nc.vector.reciprocal(inv0, total0[:])
+        total1 = reciprocals(1, recip1)
+        w_grouped = [weights(0, recip0[:], inv0, None)]
+        inv1 = sb("inv1", [P, 1], F32, "inv1")
+        nc.vector.reciprocal(inv1[:], total1[:])
+        values_plane(3)
+        w_grouped.append(weights(1, recip1, inv1[:], "place3"))
+        vq, wq = [], []
+        for n in range(2):
+            codes = sb(f"val_codes{n}", [P, 2 * P], U32, "inv1" if n == 0 else None)
+            scales = sb(f"val_scales{n}", [P, 2 * P], U8)
+            quantise(codes[:], scales[:], val_grouped[n][:])
+            vq.extend((codes[:, m * P : (m + 1) * P], scales[:, m * P : (m + 1) * P]) for m in range(2))
+            codes = sb(f"w_codes{n}", [P, P], U32, "place2" if n == 0 else None)
+            scales = sb(f"w_scales{n}", [P, P], U8)
+            quantise(codes[:], scales[:], w_grouped[n][:])
+            wq.append((codes, scales))
 
         out_rows = out_0.rearrange("(p r) q -> p r q", r=PACK)
         out_words = out_1[0].rearrange("p q r -> p (q r)").bitcast(I32)
         y_scales = sb("y_scales", [P, Q], U8)
         for j in range(HALVES):
             cols = slice(j * P, (j + 1) * P)
-            ps = bank(f"y_ps{j}", f"b{j}")
-            for r in range(PACK):
-                nc.tensor.matmul_mx(
-                    out=ps[:, r * P : (r + 1) * P],
-                    lhsT=vq[r][0].bitcast(FP8X4),
-                    lhsT_scale=vq[r][1],
-                    rhs=w_codes[:, cols].bitcast(FP8X4),
-                    rhs_scale=w_scales[:, cols],
-                    start=True,
-                    stop=True,
-                )
             y_grouped = sb(f"y_grouped{j}", [P, P, PACK], BF16)
             y = sb(f"y{j}", [P, PACK, P], F32)
-            permuted = ps[:].rearrange("p (r q) -> p q r", r=PACK)
-            if j == 0:
-                nc.vector.tensor_copy(y_grouped[:], permuted)
-                nc.scalar.copy(y[:].rearrange("p r q -> p (r q)"), ps[:])
-            else:
-                nc.scalar.copy(y_grouped[:], permuted)
-                nc.vector.tensor_copy(y[:].rearrange("p r q -> p (r q)"), ps[:])
+            groups = [range(PACK)] if j == 0 else [range(0, 2), range(2, PACK)]
+            banks = []
+            for n, planes in enumerate(groups):
+                y_ps = bank(f"y_ps{j}{n}", j + n)
+                for m, r in enumerate(planes):
+                    nc.tensor.matmul_mx(
+                        out=y_ps[:, m * P : (m + 1) * P],
+                        lhsT=vq[r][0].bitcast(FP8X4),
+                        lhsT_scale=vq[r][1],
+                        rhs=wq[j][0][:].bitcast(FP8X4),
+                        rhs_scale=wq[j][1][:],
+                        start=True,
+                        stop=True,
+                    )
+                banks.append((y_ps[:, 0 : len(planes) * P], slice(planes.start, planes.stop)))
+            for n, (held, rs) in enumerate(banks):
+                steps = [
+                    lambda: nc.vector.tensor_copy(y_grouped[:, :, rs], held.rearrange("p (r q) -> p q r", q=P)),
+                    lambda: nc.scalar.copy(y[:, rs, :].rearrange("p r q -> p (r q)"), held),
+                ]
+                for step in steps if n == 0 else reversed(steps):
+                    step()
             y_codes = sb(f"y_codes{j}", [P, P], U32)
-            nc.vector.quantize_mx(
-                out=y_codes[:].bitcast(FP8X4),
-                scales=y_scales[:, cols],
-                in_=y_grouped[:].rearrange("p q r -> p (q r)"),
-            )
-            nc.sync.dma_start(out_rows[:, :, cols], y[:])
+            quantise(y_codes[:], y_scales[:, cols], y_grouped[:].rearrange("p q r -> p (q r)"))
+            nc.scalar.dma_start(out_rows[:, :, cols], y[:])
             nc.sync.dma_start(out_words[:, cols], y_codes[:].bitcast(I32))
-        for quad in range(4):
-            queue = nc.sync if quad % 2 == 0 else nc.scalar
+        for quad in range(QUADS):
+            queue = nc.sync if quad < 3 else nc.scalar
             queue.dma_start(
                 out_2[0, 4 * quad : 4 * quad + 4, :].bitcast(I32),
                 y_scales[32 * quad : 32 * quad + 4, :].bitcast(I32),

@@ -1,7 +1,6 @@
 from contextlib import ExitStack
 
 import concourse.mybir as mybir
-from concourse.masks import make_identity
 
 D, T, I, Q, E = 512, 2048, 512, 256, 512
 FLOPS = 2 * D * Q * I + 2 * I * E * Q
@@ -22,7 +21,10 @@ PACK = 4
 BANK = 512
 HALVES = Q // P
 QUADS = 4
-KN_SPLIT = 1280
+LANDING = 160 * 1024
+WINDOW = 4 * T
+QUERIES = LANDING - WINDOW
+PAIR = 2 * WINDOW + 128
 
 
 def tile_attend_necread_pl_kernel(
@@ -33,8 +35,8 @@ def tile_attend_necread_pl_kernel(
         keep = ctx.enter_context(tc.tile_pool(name="keep", bufs=1))
         psum = ctx.enter_context(tc.psum_pool(name="psum", bufs=1))
 
-        def sb(name, shape, dtype, place=None):
-            return keep.tile(shape, dtype, name=name, tag=place or name, align_bytes=64)
+        def sb(name, shape, dtype, place=None, at=None):
+            return keep.tile(shape, dtype, name=name, tag=place or name, align_bytes=64, offset=at)
 
         def bank(name, number):
             return psum.tile([P, BANK], F32, name=name, tag=f"bank{number}")
@@ -45,105 +47,91 @@ def tile_attend_necread_pl_kernel(
         offsets = keep.tile([P, I // 16], U16, name="offsets")
         nc.sync.dma_start(offsets[:], offs)
 
-        qn_raw = sb("qn_raw", [P, HALVES], F32, "place0")
-        kn_win = sb("kn_win", [P, T], F32, "place1")
-        q_raw = sb("q_raw", [P, PACK, Q], F32, "place2")
         key_scale_win = sb("key_scale_win", [P, T], U8)
-
         nc.gpsimd.memset(key_scale_win[:].bitcast(U32), 0)
         ident = sb("ident", [P, P], F32)
-        make_identity(nc, ident[:])
+        zeros = [sb(f"zeros{h}", [P, P // 2], F32, at=LANDING + PAIR * h + WINDOW - 64) for h in range(2)]
+        for source in zeros:
+            nc.gpsimd.memset(source[:], 0.0)
+        for h, source in enumerate(zeros):
+            nc.gpsimd.affine_select(
+                out=ident[:, h * P // 2 : (h + 1) * P // 2], in_=source[:], compare_op=ALU.not_equal, fill=1.0,
+                base=-h * P // 2, pattern=[[-1, P // 2]], channel_multiplier=1,
+            )
         warm = sb("warm", [P, 1], F32)
         nc.vector.memset(warm[:], 1.0)
-        nc.vector.memset(kn_win[0 : P - 1, 0:KN_SPLIT], 0.0)
-        nc.gpsimd.memset(kn_win[0 : P - 1, KN_SPLIT:T], 0.0)
+        kn_win = sb("kn_win", [P, T], F32)
+        nc.vector.memset(kn_win[0 : P - 1, :].bitcast(I32), 0)
 
         nc.sync.dma_start(kn_win[P - 1 : P, :], kn[0:1, :])
-        with nc.allow_non_contiguous_dma(reason="one number a query row"):
-            nc.sync.dma_start(qn_raw[:], qn.rearrange("(j p) o -> p (j o)", p=P))
-        size_col = sb("size_col", [P, PACK], F32)
-        nc.sync.dma_start(size_col[:], size.rearrange("o (p t) -> p (o t)", t=PACK))
-        nc.sync.dma_start(q_raw[:], query.rearrange("(p j) q -> p j q", j=PACK))
-        key_word_win = sb("key_word_win", [P, T], U16, "place3")
+        key_word_win = sb("key_word_win", [P, T], U16)
         nc.sync.dma_start(key_word_win[:].bitcast(I32), keys_words[0].bitcast(I32))
+        q_raw = sb("q_raw", [P, PACK, Q], F32, at=QUERIES)
+        nc.sync.dma_start(q_raw[:], query.rearrange("(p j) q -> p j q", j=PACK))
         for quad in range(QUADS):
             nc.sync.dma_start(
                 key_scale_win[32 * quad : 32 * quad + 4, :].bitcast(I32),
                 keys_scales[0, 4 * quad : 4 * quad + 4, :].bitcast(I32),
             )
+        qn_raw = sb("qn_raw", [P, HALVES], F32, at=LANDING + WINDOW)
+        with nc.allow_non_contiguous_dma(reason="one number a query row"):
+            nc.sync.dma_start(qn_raw[:], qn.rearrange("(j p) o -> p (j o)", p=P))
+        vals_rows = vals.rearrange("(p r) t -> r p t", r=PACK)
+        val_at = [LANDING + PAIR * (r // 2) + (WINDOW + 128) * (r % 2) for r in range(PACK)]
+        val_wins = []
+        for r in range(PACK):
+            win = sb(f"val_win{r}", [P, T], F32, at=val_at[r])
+            nc.sync.dma_start(win[:], vals_rows[r])
+            val_wins.append(win)
+            if r == 0:
+                size_col = sb("size_col", [P, PACK], F32, at=val_at[1] - 64)
+                nc.sync.dma_start(size_col[:], size.rearrange("o (p t) -> p (o t)", t=PACK))
+
         warm_out = sb("warm_out", [P, 1], F32)
         nc.scalar.activation(warm_out[:], warm[:], ACT.Abs_reciprocal_sqrt)
         qn_col = sb("qn_col", [P, HALVES], F32)
-        nc.gpsimd.tensor_scalar_add(qn_col[:], qn_raw[:], 0.1)
+        nc.scalar.activation(qn_col[:], qn_raw[:], ACT.Copy, bias=0.1)
+
+        kn_g = sb("kn_g", [P, I], F32)
+        nc.vector.tensor_copy(kn_g[:], kn_win[:].indirect(offsets[:]))
+        key_words = sb("key_words", [P, I], U16)
+        nc.vector.tensor_copy(key_words[:], key_word_win[:].indirect(offsets[:]))
+        key_scales = sb("key_scales", [P, I], U8)
+        nc.vector.tensor_copy(key_scales[:], key_scale_win[:].indirect(offsets[:]))
 
         q_grouped = sb("q_grouped", [P, Q, PACK], BF16)
         nc.scalar.copy(
             q_grouped[:].rearrange("p (c i) j -> p c j i", i=4),
             q_raw[:].rearrange("p j (c i) -> p c j i", i=4),
         )
-
-        kn_g = sb("kn_g", [P, I], F32)
-        nc.vector.tensor_copy(kn_g[:], kn_win[:].indirect(offsets[:]))
-        key_words = sb("key_words", [P, I], U16)
-        nc.vector.tensor_copy(key_words[:], key_word_win[:].indirect(offsets[:]))
         q_codes = sb("q_codes", [P, Q], U32)
-        q_scales = sb("q_scales", [P, Q], U8)
-        key_scales = sb("key_scales", [P, I], U8)
-        for h in range(2):
-            nc.vector.tensor_copy(
-                key_scales[:, h * 2 * P : (h + 1) * 2 * P],
-                key_scale_win[:].indirect(offsets[:, 16 * h : 16 * (h + 1)]),
-            )
-            if h == 0:
-                quantise(q_codes[:], q_scales[:], q_grouped[:].rearrange("p q j -> p (q j)"))
-
-        vals_rows = vals.rearrange("(p r) t -> r p t", r=PACK)
-        val_wins = []
-        for r in range(PACK):
-            win = sb(f"val_win{r}", [P, T], F32, f"place{r}")
-            nc.sync.dma_start(win[:], vals_rows[r])
-            val_wins.append(win)
+        q_scales = sb("q_scales", [P, Q], U8, "key_scale_win")
+        quantise(q_codes[:], q_scales[:], q_grouped[:].rearrange("p q j -> p (q j)"))
 
         kn_ps = bank("kn_ps", 4)
         for c in range(4):
             nc.tensor.transpose(kn_ps[:, c * P : (c + 1) * P], kn_g[:, c * P : (c + 1) * P], ident[:])
-        kn_col = sb("kn_col", [P, 4], F32)
+        kn_col = sb("kn_col", [P, 4], F32, at=QUERIES)
         nc.scalar.copy(kn_col[:], kn_ps[:, P - 1 : BANK : P])
+
         kn_row_ps = bank("kn_row_ps", 5)
         for c in range(4):
             nc.tensor.transpose(
                 kn_row_ps[:, c * P : (c + 1) * P], kn_col[:, c : c + 1].to_broadcast([P, P]), ident[:]
             )
-        lengths = sb("lengths", [P, I], F32, "lengths")
-        nc.scalar.activation(lengths[:], kn_row_ps[:], ACT.Identity, bias=qn_col[:, 0:1])
-        size_ps = bank("size_ps", 4)
-        size_dealt = size_ps[:].rearrange("p (u s e) -> p u e s", u=2, e=2)
-        for t in range(PACK):
-            nc.tensor.transpose(
-                size_dealt[:, t // 2, t % 2, :], size_col[:, t : t + 1].to_broadcast([P, P]), ident[:]
-            )
+        kn_row = sb("kn_row", [P, I], F32)
+        nc.scalar.copy(kn_row[:], kn_row_ps[:])
 
-        part = []
+        dist0 = bank("dist0", 3)
         for h in range(2):
-            score_ps = bank(f"score_ps{h}", 1 + h)
+            score_ps = bank(f"score_ps{h}", h)
             for c in (2 * h, 2 * h + 1):
                 nc.tensor.matmul_mx(
                     out=score_ps[:, (c % 2) * P : (c % 2 + 1) * P],
                     lhsT=key_words[:, c * P : (c + 1) * P].bitcast(FP4X4),
                     lhsT_scale=key_scales[:, c * P : (c + 1) * P],
-                    rhs=q_codes[:, P:Q].bitcast(FP8X4),
-                    rhs_scale=q_scales[:, P:Q],
-                    start=True,
-                    stop=True,
-                )
-            if h == 1:
-                row_ps = bank("row_ps", 0)
-                nc.tensor.matmul_mx(
-                    out=row_ps[:],
-                    lhsT=q_codes[:, 0:P].bitcast(FP8X4),
-                    lhsT_scale=q_scales[:, 0:P],
-                    rhs=key_words[:].bitcast(FP4X4),
-                    rhs_scale=key_scales[:],
+                    rhs=q_codes[:, 0:P].bitcast(FP8X4),
+                    rhs_scale=q_scales[:, 0:P],
                     start=True,
                     stop=True,
                 )
@@ -153,18 +141,25 @@ def tile_attend_necread_pl_kernel(
                     piece[:], score_ps[:, (c % 2) * P : (c % 2 + 1) * P], ACT.Identity,
                     bias=kn_col[:, c : c + 1], scale=-2.0,
                 )
-                part.append(piece)
-
-        dist0 = sb("dist0", [P, I], F32)
-        nc.vector.scalar_tensor_tensor(dist0[:], row_ps[:], -2.0, lengths[:], ALU.mult, ALU.add)
-        dist1 = bank("dist1", 3)
-        for c in range(4):
-            nc.tensor.transpose(dist1[:, c * P : (c + 1) * P], part[c][:], ident[:])
+                nc.tensor.transpose(dist0[:, c * P : (c + 1) * P], piece[:], ident[:])
+        row_ps = bank("row_ps", 2)
+        nc.tensor.matmul_mx(
+            out=row_ps[:],
+            lhsT=q_codes[:, P:Q].bitcast(FP8X4),
+            lhsT_scale=q_scales[:, P:Q],
+            rhs=key_words[:].bitcast(FP4X4),
+            rhs_scale=key_scales[:],
+            start=True,
+            stop=True,
+        )
+        dist1 = sb("dist1", [P, I], F32, at=val_at[0])
 
         mags, signs = [], []
-        for j, (dist, bias) in enumerate(((dist0, 0.0), (dist1, qn_col[:, 1:2]))):
+
+        def magnitudes(j, dist):
+            bias = qn_col[:, j : j + 1]
             dealt = dist[:].rearrange("p (s u e) -> p u s e", u=2, e=2)
-            root = sb(f"root{j}", [P, 2, P, 2], F32, f"root{j}")
+            root = sb(f"root{j}", [P, 2, P, 2], F32)
             nc.scalar.activation(root[:], dealt, ACT.Abs_reciprocal_sqrt, bias=bias)
             sign = sb(f"sign{j}", [P, 2, P, 2], F32)
             nc.scalar.activation(sign[:], dealt, ACT.Sign, bias=bias)
@@ -173,35 +168,58 @@ def tile_attend_necread_pl_kernel(
             mags.append(mag[:].rearrange("p u s e -> p (u s e)"))
             signs.append(sign[:].rearrange("p u s e -> p (u s e)"))
 
-        val_grouped = [sb("val_grouped0", [P, 2 * I], BF16, "root1"), sb("val_grouped1", [P, 2 * I], BF16, "root0")]
-        val_ps = [bank("val_ps0", 6), bank("val_ps1", 7)]
+        magnitudes(0, dist0)
 
-        def values_plane(r):
-            picked = sb(f"val_picked{r}", [P, I], BF16, "lengths" if r == 0 else None)
-            nc.vector.tensor_copy(picked[:], val_wins[r][:].indirect(offsets[:]))
+        size_ps = bank("size_ps", 0)
+        size_dealt = size_ps[:].rearrange("p (u s e) -> p u e s", u=2, e=2)
+        for t in range(PACK):
+            nc.tensor.transpose(
+                size_dealt[:, t // 2, t % 2, :], size_col[:, t : t + 1].to_broadcast([P, P]), ident[:]
+            )
+
+        val_grouped = [sb("val_grouped01", [P, 2 * I], BF16, "root1"), sb("val_grouped2", [P, I], BF16), sb("val_grouped3", [P, I], BF16)]
+        val_ps = [bank("val_ps01", 6), bank("val_ps2", 7), bank("val_ps3", 2)]
+
+        def gather_values(r):
+            picked = sb(f"val_picked{r}", [P, I], BF16, at=QUERIES + 1024 * (r + 1) if r < 2 else None)
+            nc.vector.tensor_copy(
+                picked[:].rearrange("p (u s e) -> p s u e", u=2, e=2), val_wins[r][:].indirect(offsets[:])
+            )
             words = picked[:].bitcast(F32)
+            n, first = max(r - 1, 0), (r == 1) * 2 * P
             for u in range(2):
-                at = (2 * (r % 2) + u) * P
-                nc.tensor.transpose(val_ps[r // 2][:, at : at + P], words[:, u : 2 * P : 2], ident[:])
-            planes = {1: (0, 2), 2: (2, 3), 3: (3, 4)}.get(r)
-            if planes:
-                a, b = planes
-                held = val_ps[r // 2][:, (a % 2) * 2 * P : (a % 2 + b - a) * 2 * P]
+                nc.tensor.transpose(val_ps[n][:, first + u * P : first + (u + 1) * P], words[:, u * P : (u + 1) * P], ident[:])
+            if r > 0:
                 nc.scalar.copy(
-                    val_grouped[r // 2][:, (a % 2) * I : (a % 2 + b - a) * I].bitcast(F32).rearrange("p (r c u) -> p r c u", c=P, u=2),
-                    held.rearrange("p (r u c) -> p r c u", c=P, u=2),
+                    val_grouped[n][:].bitcast(F32).rearrange("p (r c u) -> p r c u", c=P, u=2),
+                    val_ps[n][:, 0 : first + 2 * P].rearrange("p (r u c) -> p r c u", c=P, u=2),
                 )
 
-        def reciprocals(j, recip):
-            total = sb(f"total{j}", [P, 1], F32)
-            nc.vector.scalar_tensor_tensor(recip, signs[j], 1.0, mags[j], ALU.mult, ALU.mult, accum_out=total[:])
-            return total
+        vq = []
 
-        def weights(j, recip, inv, place):
-            w = sb(f"w{j}", [P, I], BF16, place)
-            nc.vector.scalar_tensor_tensor(w[:], recip, inv, size_ps[:], ALU.mult, ALU.mult)
+        def quantise_values(n, place):
+            width = val_grouped[n].shape[1] // PACK
+            codes = sb(f"val_codes{n}", [P, width], U32, place)
+            scales = sb(f"val_scales{n}", [P, width], U8)
+            quantise(codes[:], scales[:], val_grouped[n][:])
+            vq.extend((codes[:, m : m + P], scales[:, m : m + P]) for m in range(0, width, P))
+
+        def reciprocals(j, at):
+            recip = sb(f"recip{j}", [P, I], F32)
+            total = sb(f"total{j}", [P, 1], F32, at=at)
+            nc.vector.scalar_tensor_tensor(recip[:], signs[j], 1.0, mags[j], ALU.mult, ALU.mult, accum_out=total[:])
+            return recip, total
+
+        def inverse(j, total, at):
+            inv = sb(f"inv{j}", [P, 1], F32, at=at)
+            nc.vector.reciprocal(inv[:], total[:])
+            return inv
+
+        def weights(j, recip, inv):
+            w = sb(f"w{j}", [P, I], BF16)
+            nc.vector.scalar_tensor_tensor(w[:], recip[:], inv[:], size_ps[:], ALU.mult, ALU.mult)
             words = w[:].bitcast(F32)
-            w_ps = bank(f"w_ps{j}", 3 + 2 * j)
+            w_ps = bank(f"w_ps{j}", 3 + j)
             for u in range(2):
                 nc.tensor.transpose(w_ps[:, u * P : (u + 1) * P], words[:, u * P : (u + 1) * P], ident[:])
             grouped = sb(f"w_grouped{j}", [P, P * PACK], BF16)
@@ -211,66 +229,79 @@ def tile_attend_necread_pl_kernel(
             )
             return grouped
 
-        values_plane(0)
-        values_plane(1)
-        recip0 = sb("recip0", [P, I], F32, "place1")
-        total0 = reciprocals(0, recip0[:])
-        values_plane(2)
-        shared = sb("shared", [P, I + 8], F32, "place2")
-        inv0, recip1 = shared[:, I : I + 1], shared[:, 0:I]
-        nc.vector.reciprocal(inv0, total0[:])
-        total1 = reciprocals(1, recip1)
-        w_grouped = [weights(0, recip0[:], inv0, None)]
-        inv1 = sb("inv1", [P, 1], F32, "inv1")
-        nc.vector.reciprocal(inv1[:], total1[:])
-        values_plane(3)
-        w_grouped.append(weights(1, recip1, inv1[:], "place3"))
-        vq, wq = [], []
-        for n in range(2):
-            codes = sb(f"val_codes{n}", [P, 2 * P], U32, "inv1" if n == 0 else None)
-            scales = sb(f"val_scales{n}", [P, 2 * P], U8)
-            quantise(codes[:], scales[:], val_grouped[n][:])
-            vq.extend((codes[:, m * P : (m + 1) * P], scales[:, m * P : (m + 1) * P]) for m in range(2))
-            codes = sb(f"w_codes{n}", [P, P], U32, "place2" if n == 0 else None)
-            scales = sb(f"w_scales{n}", [P, P], U8)
-            quantise(codes[:], scales[:], w_grouped[n][:])
-            wq.append((codes, scales))
+        def quantise_weights(j, grouped):
+            codes = sb(f"w_codes{j}", [P, P], U32)
+            scales = sb(f"w_scales{j}", [P, P], U8)
+            quantise(codes[:], scales[:], grouped[:])
+            return codes, scales
+
+        gather_values(0)
+        nc.vector.scalar_tensor_tensor(dist1[:], row_ps[:], -2.0, kn_row[:], ALU.mult, ALU.add)
+        magnitudes(1, dist1)
+        gather_values(1)
+        recip0, total0 = reciprocals(0, val_at[1])
+        gather_values(2)
+        inv0 = inverse(0, total0, val_at[2])
+        recip1, total1 = reciprocals(1, val_at[2] + 64)
+        w_grouped0 = weights(0, recip0, inv0)
+        inv1 = inverse(1, total1, None)
+        quantise_values(0, "sign1")
+        w_grouped1 = weights(1, recip1, inv1)
+        wq = [quantise_weights(0, w_grouped0)]
+        gather_values(3)
+        wq.append(quantise_weights(1, w_grouped1))
+        quantise_values(1, None)
+        quantise_values(2, None)
 
         out_rows = out_0.rearrange("(p r) q -> p r q", r=PACK)
         out_words = out_1[0].rearrange("p q r -> p (q r)").bitcast(I32)
+
+        def product(r, j, out):
+            nc.tensor.matmul_mx(
+                out=out,
+                lhsT=vq[r][0].bitcast(FP8X4),
+                lhsT_scale=vq[r][1],
+                rhs=wq[j][0][:].bitcast(FP8X4),
+                rhs_scale=wq[j][1][:],
+                start=True,
+                stop=True,
+            )
+
         y_scales = sb("y_scales", [P, Q], U8)
+        y_grouped = [sb(f"y_grouped{j}", [P, P, PACK], BF16) for j in range(HALVES)]
+        pair_banks = ((5, 1), (0, 3))
+
+        def products(n, j):
+            pair_ps = bank(f"y_ps{n}{j}", pair_banks[n][j])
+            for m in range(2):
+                product(2 * n + m, j, pair_ps[:, m * P : (m + 1) * P])
+            return pair_ps[:, 0 : 2 * P]
+
+        def rounded(copy, n, j, held):
+            copy(y_grouped[j][:, :, 2 * n : 2 * n + 2], held.rearrange("p (r q) -> p q r", q=P))
+
+        for j in range(HALVES):
+            held = products(0, j)
+            early = sb(f"y_early{j}", [P, 2, P], F32)
+            if j == 1:
+                rounded(nc.scalar.copy, 0, j, held)
+            nc.scalar.copy(early[:].rearrange("p r q -> p (r q)"), held)
+            nc.sync.dma_start(out_rows[:, 0:2, j * P : (j + 1) * P], early[:])
+            if j == 0:
+                rounded(nc.vector.tensor_copy, 0, j, held)
+        y_late = sb("y_late", [P, 2, Q], F32)
+        for j, copy in enumerate((nc.vector.tensor_copy, nc.scalar.copy)):
+            held = products(1, j)
+            rounded(copy, 1, j, held)
+            copy(y_late[:, :, j * P : (j + 1) * P], held.rearrange("p (r q) -> p r q", q=P))
+        nc.scalar.dma_start(out_rows[:, 2:PACK, :], y_late[:])
         for j in range(HALVES):
             cols = slice(j * P, (j + 1) * P)
-            y_grouped = sb(f"y_grouped{j}", [P, P, PACK], BF16)
-            y = sb(f"y{j}", [P, PACK, P], F32)
-            groups = [range(PACK)] if j == 0 else [range(0, 2), range(2, PACK)]
-            banks = []
-            for n, planes in enumerate(groups):
-                y_ps = bank(f"y_ps{j}{n}", j + n)
-                for m, r in enumerate(planes):
-                    nc.tensor.matmul_mx(
-                        out=y_ps[:, m * P : (m + 1) * P],
-                        lhsT=vq[r][0].bitcast(FP8X4),
-                        lhsT_scale=vq[r][1],
-                        rhs=wq[j][0][:].bitcast(FP8X4),
-                        rhs_scale=wq[j][1][:],
-                        start=True,
-                        stop=True,
-                    )
-                banks.append((y_ps[:, 0 : len(planes) * P], slice(planes.start, planes.stop)))
-            for n, (held, rs) in enumerate(banks):
-                steps = [
-                    lambda: nc.vector.tensor_copy(y_grouped[:, :, rs], held.rearrange("p (r q) -> p q r", q=P)),
-                    lambda: nc.scalar.copy(y[:, rs, :].rearrange("p r q -> p (r q)"), held),
-                ]
-                for step in steps if n == 0 else reversed(steps):
-                    step()
             y_codes = sb(f"y_codes{j}", [P, P], U32)
-            quantise(y_codes[:], y_scales[:, cols], y_grouped[:].rearrange("p q r -> p (q r)"))
-            nc.scalar.dma_start(out_rows[:, :, cols], y[:])
+            quantise(y_codes[:], y_scales[:, cols], y_grouped[j][:].rearrange("p q r -> p (q r)"))
             nc.sync.dma_start(out_words[:, cols], y_codes[:].bitcast(I32))
         for quad in range(QUADS):
-            queue = nc.sync if quad < 3 else nc.scalar
+            queue = nc.sync if quad < 2 else nc.scalar
             queue.dma_start(
                 out_2[0, 4 * quad : 4 * quad + 4, :].bitcast(I32),
                 y_scales[32 * quad : 32 * quad + 4, :].bitcast(I32),

@@ -70,8 +70,8 @@ def tile_attend_necread_pl_kernel(
         nc.sync.dma_start(q_raw[:], query.rearrange("(p j) q -> p j q", j=PACK))
         for quad in range(QUADS):
             nc.sync.dma_start(
-                key_scale_win[32 * quad : 32 * quad + 4, :].bitcast(I32),
-                keys_scales[0, 4 * quad : 4 * quad + 4, :].bitcast(I32),
+                key_scale_win[quad:P:32, :].bitcast(I32),
+                keys_scales[0, quad:16:4, :].bitcast(I32),
             )
         qn_raw = sb("qn_raw", [P, HALVES], F32, at=LANDING + WINDOW)
         with nc.allow_non_contiguous_dma(reason="one number a query row"):

@@ -268,6 +268,7 @@ def tile_attend_necread_pl_kernel(
             )
 
         y_scales = sb("y_scales", [P, Q], U8)
+        y_codes = sb("y_codes", [P, Q], U32)
         y_grouped = [sb(f"y_grouped{j}", [P, P, PACK], BF16) for j in range(HALVES)]
         pair_banks = ((5, 1), (0, 3))
 
@@ -297,9 +298,8 @@ def tile_attend_necread_pl_kernel(
         nc.scalar.dma_start(out_rows[:, 2:PACK, :], y_late[:])
         for j in range(HALVES):
             cols = slice(j * P, (j + 1) * P)
-            y_codes = sb(f"y_codes{j}", [P, P], U32)
-            quantise(y_codes[:], y_scales[:, cols], y_grouped[j][:].rearrange("p q r -> p (q r)"))
-            nc.sync.dma_start(out_words[:, cols], y_codes[:].bitcast(I32))
+            quantise(y_codes[:, cols], y_scales[:, cols], y_grouped[j][:].rearrange("p q r -> p (q r)"))
+        nc.sync.dma_start(out_words, y_codes[:].bitcast(I32))
         for quad in range(QUADS):
             queue = nc.sync if quad < 2 else nc.scalar
             queue.dma_start(

@@ -25,6 +25,8 @@ LANDING = 160 * 1024
 WINDOW = 4 * T
 QUERIES = LANDING - WINDOW
 PAIR = 2 * WINDOW + 128
+SPLIT = 1280
+SHARES = ((0, SPLIT), (SPLIT, T))
 
 
 def tile_attend_necread_pl_kernel(
@@ -50,13 +52,14 @@ def tile_attend_necread_pl_kernel(
         key_scale_win = sb("key_scale_win", [P, T], U8)
         nc.gpsimd.memset(key_scale_win[:].bitcast(U32), 0)
         ident = sb("ident", [P, P], F32)
-        zeros = [sb(f"zeros{h}", [P, P // 2], F32, at=LANDING + PAIR * h + WINDOW - 64) for h in range(2)]
+        spans = ((0, 64, LANDING + WINDOW - 64), (64, 96, LANDING + PAIR + 4 * SPLIT - 64), (96, 128, LANDING + PAIR + WINDOW + 128))
+        zeros = [sb(f"zeros{a}", [P, b - a], F32, at=at) for a, b, at in spans]
         for source in zeros:
             nc.gpsimd.memset(source[:], 0.0)
-        for h, source in enumerate(zeros):
+        for (a, b, at), source in zip(spans, zeros):
             nc.gpsimd.affine_select(
-                out=ident[:, h * P // 2 : (h + 1) * P // 2], in_=source[:], compare_op=ALU.not_equal, fill=1.0,
-                base=-h * P // 2, pattern=[[-1, P // 2]], channel_multiplier=1,
+                out=ident[:, a:b], in_=source[:], compare_op=ALU.not_equal, fill=1.0,
+                base=-a, pattern=[[-1, b - a]], channel_multiplier=1,
             )
         warm = sb("warm", [P, 1], F32)
         nc.vector.memset(warm[:], 1.0)
@@ -80,8 +83,13 @@ def tile_attend_necread_pl_kernel(
         val_at = [LANDING + PAIR * (r // 2) + (WINDOW + 128) * (r % 2) for r in range(PACK)]
         val_wins = []
         for r in range(PACK):
-            win = sb(f"val_win{r}", [P, T], F32, at=val_at[r])
-            nc.sync.dma_start(win[:], vals_rows[r])
+            if r == 2:
+                win = [sb(f"val_win2{a}", [P, b - a], F32, at=val_at[r] + 4 * a) for a, b in SHARES]
+                for share, (a, b) in zip(win, SHARES):
+                    nc.sync.dma_start(share[:], vals_rows[r][:, a:b])
+            else:
+                win = sb(f"val_win{r}", [P, T], F32, at=val_at[r])
+                nc.sync.dma_start(win[:], vals_rows[r])
             val_wins.append(win)
             if r == 0:
                 size_col = sb("size_col", [P, PACK], F32, at=val_at[1] - 64)
@@ -161,12 +169,13 @@ def tile_attend_necread_pl_kernel(
             dealt = dist[:].rearrange("p (s u e) -> p u s e", u=2, e=2)
             root = sb(f"root{j}", [P, 2, P, 2], F32)
             nc.scalar.activation(root[:], dealt, ACT.Abs_reciprocal_sqrt, bias=bias)
-            sign = sb(f"sign{j}", [P, 2, P, 2], F32)
-            nc.scalar.activation(sign[:], dealt, ACT.Sign, bias=bias)
+            if j == 0:
+                sign = sb("sign0", [P, 2, P, 2], F32)
+                nc.scalar.activation(sign[:], dealt, ACT.Sign, bias=bias)
+                signs.append(sign[:].rearrange("p u s e -> p (u s e)"))
             mag = sb(f"mag{j}", [P, 2, P, 2], F32)
             nc.scalar.activation(mag[:], root[:], ACT.Square)
             mags.append(mag[:].rearrange("p u s e -> p (u s e)"))
-            signs.append(sign[:].rearrange("p u s e -> p (u s e)"))
 
         magnitudes(0, dist0)
 
@@ -178,13 +187,21 @@ def tile_attend_necread_pl_kernel(
             )
 
         val_grouped = [sb("val_grouped01", [P, 2 * I], BF16, "root1"), sb("val_grouped2", [P, I], BF16), sb("val_grouped3", [P, I], BF16)]
-        val_ps = [bank("val_ps01", 6), bank("val_ps2", 7), bank("val_ps3", 2)]
+        val_ps = [bank("val_ps01", 6), bank("val_ps2", 0), bank("val_ps3", 2)]
 
         def gather_values(r):
             picked = sb(f"val_picked{r}", [P, I], BF16, at=QUERIES + 1024 * (r + 1) if r < 2 else None)
-            nc.vector.tensor_copy(
-                picked[:].rearrange("p (u s e) -> p s u e", u=2, e=2), val_wins[r][:].indirect(offsets[:])
-            )
+            dealt = picked[:].rearrange("p (u s e) -> p s u e", u=2, e=2)
+            if r == 2:
+                rounded_win = sb("val_rounded2", [P, T], BF16)
+                nc.vector.tensor_copy(rounded_win[:, 0:SPLIT], val_wins[r][0][:])
+                nc.scalar.activation(rounded_win[:, SPLIT:T], val_wins[r][1][:], ACT.Copy)
+                nc.scalar.activation(dealt, rounded_win[:].indirect(offsets[:]), ACT.Copy)
+            else:
+                nc.vector.tensor_copy(dealt, val_wins[r][:].indirect(offsets[:]))
+            return picked
+
+        def turn_values(r, picked):
             words = picked[:].bitcast(F32)
             n, first = max(r - 1, 0), (r == 1) * 2 * P
             for u in range(2):
@@ -199,7 +216,7 @@ def tile_attend_necread_pl_kernel(
 
         def quantise_values(n, place):
             width = val_grouped[n].shape[1] // PACK
-            codes = sb(f"val_codes{n}", [P, width], U32, place)
+            codes = sb(f"val_codes{n}", [P, width], U32, place, at=val_at[3] + 1024 if n == 1 else None)
             scales = sb(f"val_scales{n}", [P, width], U8)
             quantise(codes[:], scales[:], val_grouped[n][:])
             vq.extend((codes[:, m : m + P], scales[:, m : m + P]) for m in range(0, width, P))
@@ -207,7 +224,9 @@ def tile_attend_necread_pl_kernel(
         def reciprocals(j, at):
             recip = sb(f"recip{j}", [P, I], F32)
             total = sb(f"total{j}", [P, 1], F32, at=at)
-            nc.vector.scalar_tensor_tensor(recip[:], signs[j], 1.0, mags[j], ALU.mult, ALU.mult, accum_out=total[:])
+            nc.vector.scalar_tensor_tensor(
+                recip[:], signs[j], -0.5 * j, mags[j], ALU.add, ALU.mult, accum_out=total[:]
+            )
             return recip, total
 
         def inverse(j, total, at):
@@ -230,25 +249,31 @@ def tile_attend_necread_pl_kernel(
             return grouped
 
         def quantise_weights(j, grouped):
-            codes = sb(f"w_codes{j}", [P, P], U32)
+            codes = sb(f"w_codes{j}", [P, P], U32, at=val_at[3] if j == 0 else None)
             scales = sb(f"w_scales{j}", [P, P], U8)
             quantise(codes[:], scales[:], grouped[:])
             return codes, scales
 
-        gather_values(0)
+        turn_values(0, gather_values(0))
         nc.vector.scalar_tensor_tensor(dist1[:], row_ps[:], -2.0, kn_row[:], ALU.mult, ALU.add)
         magnitudes(1, dist1)
-        gather_values(1)
+        turn_values(1, gather_values(1))
+        above = sb("sign1", [P, 2, P, 2], F32, at=val_at[1] + 1024)
+        nc.vector.tensor_scalar(
+            above[:], dist1[:].rearrange("p (s u e) -> p u s e", u=2, e=2), qn_col[:, 1:2], 0.0, ALU.add, ALU.is_ge
+        )
+        signs.append(above[:].rearrange("p u s e -> p (u s e)"))
         recip0, total0 = reciprocals(0, val_at[1])
-        gather_values(2)
+        picked2 = gather_values(2)
         inv0 = inverse(0, total0, val_at[2])
         recip1, total1 = reciprocals(1, val_at[2] + 64)
         w_grouped0 = weights(0, recip0, inv0)
         inv1 = inverse(1, total1, None)
-        quantise_values(0, "sign1")
+        quantise_values(0, "mag1")
         w_grouped1 = weights(1, recip1, inv1)
         wq = [quantise_weights(0, w_grouped0)]
-        gather_values(3)
+        turn_values(2, picked2)
+        turn_values(3, gather_values(3))
         wq.append(quantise_weights(1, w_grouped1))
         quantise_values(1, None)
         quantise_values(2, None)
@@ -270,7 +295,7 @@ def tile_attend_necread_pl_kernel(
         y_scales = sb("y_scales", [P, Q], U8)
         y_codes = sb("y_codes", [P, Q], U32)
         y_grouped = [sb(f"y_grouped{j}", [P, P, PACK], BF16) for j in range(HALVES)]
-        pair_banks = ((5, 1), (0, 3))
+        pair_banks = ((5, 1), (7, 3))
 
         def products(n, j):
             pair_ps = bank(f"y_ps{n}{j}", pair_banks[n][j])

@@ -24,9 +24,13 @@ QUADS = 4
 LANDING = 160 * 1024
 WINDOW = 4 * T
 QUERIES = LANDING - WINDOW
-PAIR = 2 * WINDOW + 128
-SPLIT = 1280
-SHARES = ((0, SPLIT), (SPLIT, T))
+KN_ROW = QUERIES
+KN_LISTED = QUERIES - 8 * I
+ROOTS = QUERIES - 24 * I
+CODES = QUERIES - 12 * I
+RECIP = QUERIES - 32 * I
+LAST = QUERIES - 36 * I
+SHARE = 256
 
 
 def tile_attend_necread_pl_kernel(
@@ -49,10 +53,11 @@ def tile_attend_necread_pl_kernel(
         offsets = keep.tile([P, I // 16], U16, name="offsets")
         nc.sync.dma_start(offsets[:], offs)
 
+        val_at = [LANDING + (WINDOW + 128) * r for r in range(PACK)]
         key_scale_win = sb("key_scale_win", [P, T], U8)
         nc.gpsimd.memset(key_scale_win[:].bitcast(U32), 0)
         ident = sb("ident", [P, P], F32)
-        spans = ((0, 64, LANDING + WINDOW - 64), (64, 96, LANDING + PAIR + 4 * SPLIT - 64), (96, 128, LANDING + PAIR + WINDOW + 128))
+        spans = ((0, 48, LANDING - 128), (48, 80, val_at[1]), (80, 104, val_at[2] + 1024), (104, 128, val_at[3]))
         zeros = [sb(f"zeros{a}", [P, b - a], F32, at=at) for a, b, at in spans]
         for source in zeros:
             nc.gpsimd.memset(source[:], 0.0)
@@ -76,108 +81,99 @@ def tile_attend_necread_pl_kernel(
                 key_scale_win[quad:P:32, :].bitcast(I32),
                 keys_scales[0, quad:16:4, :].bitcast(I32),
             )
-        qn_raw = sb("qn_raw", [P, HALVES], F32, at=LANDING + WINDOW)
-        with nc.allow_non_contiguous_dma(reason="one number a query row"):
-            nc.sync.dma_start(qn_raw[:], qn.rearrange("(j p) o -> p (j o)", p=P))
+        picked0 = sb("val_picked0", [P, I + 32], BF16, at=LANDING - 128 - 2 * I)
+        qn_col = picked0[:].bitcast(F32)[:, I // 2 - 1 : I // 2 + 1]
         vals_rows = vals.rearrange("(p r) t -> r p t", r=PACK)
-        val_at = [LANDING + PAIR * (r // 2) + (WINDOW + 128) * (r % 2) for r in range(PACK)]
         val_wins = []
         for r in range(PACK):
-            if r == 2:
-                win = [sb(f"val_win2{a}", [P, b - a], F32, at=val_at[r] + 4 * a) for a, b in SHARES]
-                for share, (a, b) in zip(win, SHARES):
-                    nc.sync.dma_start(share[:], vals_rows[r][:, a:b])
-            else:
-                win = sb(f"val_win{r}", [P, T], F32, at=val_at[r])
-                nc.sync.dma_start(win[:], vals_rows[r])
+            win = sb(f"val_win{r}", [P, T], F32, at=val_at[r])
+            nc.sync.dma_start(win[:], vals_rows[r])
             val_wins.append(win)
             if r == 0:
-                size_col = sb("size_col", [P, PACK], F32, at=val_at[1] - 64)
+                with nc.allow_non_contiguous_dma(reason="one number a query row"):
+                    nc.sync.dma_start(qn_col, qn.rearrange("(j p) o -> p (j o)", p=P))
+                size_col = sb("size_col", [P, PACK], F32, at=LANDING - 64)
                 nc.sync.dma_start(size_col[:], size.rearrange("o (p t) -> p (o t)", t=PACK))
 
         warm_out = sb("warm_out", [P, 1], F32)
         nc.scalar.activation(warm_out[:], warm[:], ACT.Abs_reciprocal_sqrt)
-        qn_col = sb("qn_col", [P, HALVES], F32)
-        nc.scalar.activation(qn_col[:], qn_raw[:], ACT.Copy, bias=0.1)
 
-        kn_g = sb("kn_g", [P, I], F32)
-        nc.vector.tensor_copy(kn_g[:], kn_win[:].indirect(offsets[:]))
+        kn_g = sb("kn_g", [P, I], F32, at=KN_LISTED)
+        nc.vector.tensor_copy(kn_g[:, 0:SHARE], kn_win[:].indirect(offsets[:, 0 : SHARE // 16]))
+        nc.scalar.activation(kn_g[:, SHARE:I], kn_win[:].indirect(offsets[:, SHARE // 16 : I // 16]), ACT.Copy)
         key_words = sb("key_words", [P, I], U16)
         nc.vector.tensor_copy(key_words[:], key_word_win[:].indirect(offsets[:]))
         key_scales = sb("key_scales", [P, I], U8)
-        nc.vector.tensor_copy(key_scales[:], key_scale_win[:].indirect(offsets[:]))
 
-        q_grouped = sb("q_grouped", [P, Q, PACK], BF16)
-        nc.scalar.copy(
-            q_grouped[:].rearrange("p (c i) j -> p c j i", i=4),
-            q_raw[:].rearrange("p j (c i) -> p c j i", i=4),
-        )
-        q_codes = sb("q_codes", [P, Q], U32)
-        q_scales = sb("q_scales", [P, Q], U8, "key_scale_win")
-        quantise(q_codes[:], q_scales[:], q_grouped[:].rearrange("p q j -> p (q j)"))
-
-        kn_ps = bank("kn_ps", 4)
+        kn_ps = bank("kn_ps", 2)
         for c in range(4):
             nc.tensor.transpose(kn_ps[:, c * P : (c + 1) * P], kn_g[:, c * P : (c + 1) * P], ident[:])
-        kn_col = sb("kn_col", [P, 4], F32, at=QUERIES)
-        nc.scalar.copy(kn_col[:], kn_ps[:, P - 1 : BANK : P])
+        kn_col = picked0[:].bitcast(F32)[:, 0:4]
+        nc.scalar.copy(kn_col, kn_ps[:, P - 1 : BANK : P])
 
-        kn_row_ps = bank("kn_row_ps", 5)
+        q_codes = sb("q_codes", [P, Q], U32, at=CODES)
+        q_scales = []
+        for j in range(HALVES):
+            nc.vector.tensor_copy(
+                key_scales[:, j * SHARE : (j + 1) * SHARE],
+                key_scale_win[:].indirect(offsets[:, j * SHARE // 16 : (j + 1) * SHARE // 16]),
+            )
+            q_scales.append(sb(f"q_scales{j}", [P, P], U8, "key_scale_win" if j == 1 else None))
+            q_grouped = sb(f"q_grouped{j}", [P, P, PACK], BF16, at=KN_LISTED + 2 * I * j)
+            nc.scalar.copy(
+                q_grouped[:].rearrange("p (c i) j -> p c j i", i=4),
+                q_raw[:, :, j * P : (j + 1) * P].rearrange("p j (c i) -> p c j i", i=4),
+            )
+            quantise(q_codes[:, j * P : (j + 1) * P], q_scales[j][:], q_grouped[:].rearrange("p q j -> p (q j)"))
+
+        kn_row_ps = bank("kn_row_ps", 3)
         for c in range(4):
             nc.tensor.transpose(
                 kn_row_ps[:, c * P : (c + 1) * P], kn_col[:, c : c + 1].to_broadcast([P, P]), ident[:]
             )
-        kn_row = sb("kn_row", [P, I], F32)
-        nc.scalar.copy(kn_row[:], kn_row_ps[:])
+        kn_row = sb("kn_row", [P, I], F32, at=KN_ROW)
+        nc.scalar.activation(kn_row[:], kn_row_ps[:], ACT.Copy, bias=0.1)
 
-        dist0 = bank("dist0", 3)
-        for h in range(2):
-            score_ps = bank(f"score_ps{h}", h)
-            for c in (2 * h, 2 * h + 1):
+        val_ps = [bank("val_ps01", 2), bank("val_ps2", 3), bank("val_ps3", 7)]
+
+        def gather_values(r, share, picked):
+            nc.scalar.activation(picked[:, 0:share], val_wins[r][:].indirect(offsets[:, 0 : share // 16]), ACT.Copy)
+            if share < I:
+                nc.vector.tensor_copy(picked[:, share:I], val_wins[r][:].indirect(offsets[:, share // 16 : I // 16]))
+            words = picked.bitcast(F32)
+            n, first = max(r - 1, 0), (r == 1) * 2 * P
+            for u in range(2):
+                nc.tensor.transpose(val_ps[n][:, first + u * P : first + (u + 1) * P], words[:, u : 2 * P : 2], ident[:])
+
+        dists = []
+        for j in range(HALVES):
+            score_ps = bank(f"score_ps{j}", j)
+            for slots in (slice(0, SHARE), slice(SHARE, I)) if j == 0 else (slice(0, I),):
                 nc.tensor.matmul_mx(
-                    out=score_ps[:, (c % 2) * P : (c % 2 + 1) * P],
-                    lhsT=key_words[:, c * P : (c + 1) * P].bitcast(FP4X4),
-                    lhsT_scale=key_scales[:, c * P : (c + 1) * P],
-                    rhs=q_codes[:, 0:P].bitcast(FP8X4),
-                    rhs_scale=q_scales[:, 0:P],
+                    out=score_ps[:, slots],
+                    lhsT=q_codes[:, j * P : (j + 1) * P].bitcast(FP8X4),
+                    lhsT_scale=q_scales[j][:],
+                    rhs=key_words[:, slots].bitcast(FP4X4),
+                    rhs_scale=key_scales[:, slots],
                     start=True,
                     stop=True,
                 )
-            for c in (2 * h, 2 * h + 1):
-                piece = sb(f"part{c}", [P, P], F32)
-                nc.scalar.activation(
-                    piece[:], score_ps[:, (c % 2) * P : (c % 2 + 1) * P], ACT.Identity,
-                    bias=kn_col[:, c : c + 1], scale=-2.0,
-                )
-                nc.tensor.transpose(dist0[:, c * P : (c + 1) * P], piece[:], ident[:])
-        row_ps = bank("row_ps", 2)
-        nc.tensor.matmul_mx(
-            out=row_ps[:],
-            lhsT=q_codes[:, P:Q].bitcast(FP8X4),
-            lhsT_scale=q_scales[:, P:Q],
-            rhs=key_words[:].bitcast(FP4X4),
-            rhs_scale=key_scales[:],
-            start=True,
-            stop=True,
-        )
-        dist1 = sb("dist1", [P, I], F32, at=val_at[0])
+            dist = sb(f"dist{j}", [P, I], F32)
+            nc.vector.scalar_tensor_tensor(dist[:], score_ps[:], -2.0, kn_row[:], ALU.mult, ALU.add)
+            dists.append(dist[:].rearrange("p (s u e) -> p u s e", u=2, e=2))
 
-        mags, signs = [], []
-
-        def magnitudes(j, dist):
-            bias = qn_col[:, j : j + 1]
-            dealt = dist[:].rearrange("p (s u e) -> p u s e", u=2, e=2)
-            root = sb(f"root{j}", [P, 2, P, 2], F32)
-            nc.scalar.activation(root[:], dealt, ACT.Abs_reciprocal_sqrt, bias=bias)
-            if j == 0:
-                sign = sb("sign0", [P, 2, P, 2], F32)
-                nc.scalar.activation(sign[:], dealt, ACT.Sign, bias=bias)
-                signs.append(sign[:].rearrange("p u s e -> p (u s e)"))
+        roots, mags, signs = [], [], []
+        for j in range(HALVES):
+            above = sb(f"above{j}", [P, 2, P, 2], BF16, at=CODES if j == 0 else None)
+            nc.vector.tensor_scalar(above[:], dists[j], qn_col[:, j : j + 1], 0.0, ALU.add, ALU.is_ge)
+            signs.append(above[:].rearrange("p u s e -> p (u s e)"))
+            root = sb(f"root{j}", [P, 2, P, 2], F32, at=ROOTS + 4 * I * j)
+            nc.scalar.activation(root[:], dists[j], ACT.Abs_reciprocal_sqrt, bias=qn_col[:, j : j + 1])
+            roots.append(root)
+        for j in range(HALVES):
             mag = sb(f"mag{j}", [P, 2, P, 2], F32)
-            nc.scalar.activation(mag[:], root[:], ACT.Square)
+            nc.scalar.activation(mag[:], roots[j][:], ACT.Square)
             mags.append(mag[:].rearrange("p u s e -> p (u s e)"))
-
-        magnitudes(0, dist0)
 
         size_ps = bank("size_ps", 0)
         size_dealt = size_ps[:].rearrange("p (u s e) -> p u e s", u=2, e=2)
@@ -186,97 +182,77 @@ def tile_attend_necread_pl_kernel(
                 size_dealt[:, t // 2, t % 2, :], size_col[:, t : t + 1].to_broadcast([P, P]), ident[:]
             )
 
-        val_grouped = [sb("val_grouped01", [P, 2 * I], BF16, "root1"), sb("val_grouped2", [P, I], BF16), sb("val_grouped3", [P, I], BF16)]
-        val_ps = [bank("val_ps01", 6), bank("val_ps2", 0), bank("val_ps3", 2)]
-
-        def gather_values(r):
-            picked = sb(f"val_picked{r}", [P, I], BF16, at=QUERIES + 1024 * (r + 1) if r < 2 else None)
-            dealt = picked[:].rearrange("p (u s e) -> p s u e", u=2, e=2)
-            if r == 2:
-                rounded_win = sb("val_rounded2", [P, T], BF16)
-                nc.vector.tensor_copy(rounded_win[:, 0:SPLIT], val_wins[r][0][:])
-                nc.scalar.activation(rounded_win[:, SPLIT:T], val_wins[r][1][:], ACT.Copy)
-                nc.scalar.activation(dealt, rounded_win[:].indirect(offsets[:]), ACT.Copy)
-            else:
-                nc.vector.tensor_copy(dealt, val_wins[r][:].indirect(offsets[:]))
-            return picked
-
-        def turn_values(r, picked):
-            words = picked[:].bitcast(F32)
-            n, first = max(r - 1, 0), (r == 1) * 2 * P
-            for u in range(2):
-                nc.tensor.transpose(val_ps[n][:, first + u * P : first + (u + 1) * P], words[:, u * P : (u + 1) * P], ident[:])
-            if r > 0:
-                nc.scalar.copy(
-                    val_grouped[n][:].bitcast(F32).rearrange("p (r c u) -> p r c u", c=P, u=2),
-                    val_ps[n][:, 0 : first + 2 * P].rearrange("p (r u c) -> p r c u", c=P, u=2),
-                )
-
         vq = []
 
-        def quantise_values(n, place):
-            width = val_grouped[n].shape[1] // PACK
-            codes = sb(f"val_codes{n}", [P, width], U32, place, at=val_at[3] + 1024 if n == 1 else None)
-            scales = sb(f"val_scales{n}", [P, width], U8)
-            quantise(codes[:], scales[:], val_grouped[n][:])
-            vq.extend((codes[:, m : m + P], scales[:, m : m + P]) for m in range(0, width, P))
-
-        def reciprocals(j, at):
-            recip = sb(f"recip{j}", [P, I], F32)
-            total = sb(f"total{j}", [P, 1], F32, at=at)
-            nc.vector.scalar_tensor_tensor(
-                recip[:], signs[j], -0.5 * j, mags[j], ALU.add, ALU.mult, accum_out=total[:]
-            )
-            return recip, total
-
-        def inverse(j, total, at):
-            inv = sb(f"inv{j}", [P, 1], F32, at=at)
-            nc.vector.reciprocal(inv[:], total[:])
-            return inv
-
-        def weights(j, recip, inv):
-            w = sb(f"w{j}", [P, I], BF16)
-            nc.vector.scalar_tensor_tensor(w[:], recip[:], inv[:], size_ps[:], ALU.mult, ALU.mult)
-            words = w[:].bitcast(F32)
-            w_ps = bank(f"w_ps{j}", 3 + j)
-            for u in range(2):
-                nc.tensor.transpose(w_ps[:, u * P : (u + 1) * P], words[:, u * P : (u + 1) * P], ident[:])
-            grouped = sb(f"w_grouped{j}", [P, P * PACK], BF16)
-            nc.scalar.copy(
-                grouped[:].bitcast(F32).rearrange("p (c u) -> p c u", u=2),
-                w_ps[:, 0 : 2 * P].rearrange("p (u c) -> p c u", u=2),
+        def group_values(n, planes, copy, at):
+            grouped = sb(f"val_grouped{n}", [P, planes * I], BF16, at=at)
+            copy(
+                grouped[:].bitcast(F32).rearrange("p (r c u) -> p r c u", c=P, u=2),
+                val_ps[n][:, 0 : planes * 2 * P].rearrange("p (r u c) -> p r c u", c=P, u=2),
             )
             return grouped
 
-        def quantise_weights(j, grouped):
-            codes = sb(f"w_codes{j}", [P, P], U32, at=val_at[3] if j == 0 else None)
-            scales = sb(f"w_scales{j}", [P, P], U8)
+        def quantise_values(n, grouped, at):
+            width = grouped.shape[1] // PACK
+            codes = sb(f"val_codes{n}", [P, width], U32, at=at)
+            scales = sb(f"val_scales{n}", [P, width], U8)
             quantise(codes[:], scales[:], grouped[:])
+            vq.extend((codes[:, m : m + P], scales[:, m : m + P]) for m in range(0, width, P))
+
+        def reciprocals(j, at):
+            recip = sb(f"recip{j}", [P, I], F32, at=at)
+            nc.vector.scalar_tensor_tensor(recip[:], signs[j], -0.5, mags[j], ALU.add, ALU.mult, accum_out=totals[:, j : j + 1])
+            return recip
+
+
+        def weights(j, recip, inv):
+            w = sb(f"w{j}", [P, I], BF16, at=val_at[1] + 12 * I if j == 0 else None)
+            nc.vector.scalar_tensor_tensor(w[:], recip[:], inv, size_ps[:], ALU.mult, ALU.mult)
+            words = w[:].bitcast(F32)
+            w_ps = bank(f"w_ps{j}", 4 - 3 * j)
+            for u in range(2):
+                nc.tensor.transpose(w_ps[:, u * P : (u + 1) * P], words[:, u * P : (u + 1) * P], ident[:])
+            return w_ps
+
+        def group_weights(w_ps, grouped, copy):
+            copy(
+                grouped.bitcast(F32).rearrange("p (c u) -> p c u", u=2),
+                w_ps[:, 0 : 2 * P].rearrange("p (u c) -> p c u", u=2),
+            )
+
+        def quantise_weights(j, grouped):
+            codes = sb(f"w_codes{j}", [P, P], U32, at=val_at[3] + 4 * I if j == 0 else None)
+            scales = sb(f"w_scales{j}", [P, P], U8)
+            quantise(codes[:], scales[:], grouped)
             return codes, scales
 
-        turn_values(0, gather_values(0))
-        nc.vector.scalar_tensor_tensor(dist1[:], row_ps[:], -2.0, kn_row[:], ALU.mult, ALU.add)
-        magnitudes(1, dist1)
-        turn_values(1, gather_values(1))
-        above = sb("sign1", [P, 2, P, 2], F32, at=val_at[1] + 1024)
-        nc.vector.tensor_scalar(
-            above[:], dist1[:].rearrange("p (s u e) -> p u s e", u=2, e=2), qn_col[:, 1:2], 0.0, ALU.add, ALU.is_ge
-        )
-        signs.append(above[:].rearrange("p u s e -> p (u s e)"))
-        recip0, total0 = reciprocals(0, val_at[1])
-        picked2 = gather_values(2)
-        inv0 = inverse(0, total0, val_at[2])
-        recip1, total1 = reciprocals(1, val_at[2] + 64)
-        w_grouped0 = weights(0, recip0, inv0)
-        inv1 = inverse(1, total1, None)
-        quantise_values(0, "mag1")
-        w_grouped1 = weights(1, recip1, inv1)
-        wq = [quantise_weights(0, w_grouped0)]
-        turn_values(2, picked2)
-        turn_values(3, gather_values(3))
-        wq.append(quantise_weights(1, w_grouped1))
-        quantise_values(1, None)
-        quantise_values(2, None)
+        gather_values(0, SHARE, picked0[:, 0:I])
+        totals = sb("totals", [P, HALVES], F32)
+        recip0 = reciprocals(0, RECIP)
+        recip1 = reciprocals(1, None)
+        inv0 = sb("inv0", [P, 1], F32)
+        nc.vector.reciprocal(inv0[:], totals[:, 0:1])
+        picked1 = sb("val_picked1", [P, I], BF16, at=ROOTS)
+        gather_values(1, 320, picked1[:])
+        inv1 = sb("inv1", [P, 1], F32, at=val_at[1])
+        nc.vector.reciprocal(inv1[:], totals[:, 1:2])
+        picked2 = sb("val_picked2", [P, I], BF16, at=ROOTS + 4 * I)
+        gather_values(2, I, picked2[:])
+        w_ps0 = weights(0, recip0, inv0[:])
+        w_ps1 = weights(1, recip1, inv1[:])
+        grouped01 = group_values(0, 2, nc.scalar.copy, val_at[2] + 8 * I)
+        w_grouped = [sb(f"w_grouped{j}", [P, I], BF16, at=val_at[3] if j == 1 else None)[:] for j in range(HALVES)]
+        group_weights(w_ps0, w_grouped[0], nc.vector.tensor_copy)
+        picked3 = sb("val_picked3", [P, I], BF16, at=RECIP + 3 * I)
+        gather_values(3, 288, picked3[:])
+        quantise_values(0, grouped01, val_at[3] + 6 * I)
+        wq = [quantise_weights(0, w_grouped[0])]
+        group_weights(w_ps1, w_grouped[1], nc.scalar.copy)
+        grouped2 = group_values(1, 1, nc.scalar.copy, val_at[3] + 2 * I)
+        grouped3 = group_values(2, 1, nc.scalar.copy, None)
+        wq.append(quantise_weights(1, w_grouped[1]))
+        quantise_values(1, grouped2, None)
+        quantise_values(2, grouped3, LAST)
 
         out_rows = out_0.rearrange("(p r) q -> p r q", r=PACK)
         out_words = out_1[0].rearrange("p q r -> p (q r)").bitcast(I32)
@@ -294,8 +270,8 @@ def tile_attend_necread_pl_kernel(
 
         y_scales = sb("y_scales", [P, Q], U8)
         y_codes = sb("y_codes", [P, Q], U32)
-        y_grouped = [sb(f"y_grouped{j}", [P, P, PACK], BF16) for j in range(HALVES)]
-        pair_banks = ((5, 1), (7, 3))
+        y_grouped = sb("y_grouped", [P, Q, PACK], BF16, at=RECIP + 4 * I)
+        pair_banks = ((5, 6), (2, 0))
 
         def products(n, j):
             pair_ps = bank(f"y_ps{n}{j}", pair_banks[n][j])
@@ -304,26 +280,28 @@ def tile_attend_necread_pl_kernel(
             return pair_ps[:, 0 : 2 * P]
 
         def rounded(copy, n, j, held):
-            copy(y_grouped[j][:, :, 2 * n : 2 * n + 2], held.rearrange("p (r q) -> p q r", q=P))
+            copy(y_grouped[:, j * P : (j + 1) * P, 2 * n : 2 * n + 2], held.rearrange("p (r q) -> p q r", q=P))
 
-        for j in range(HALVES):
-            held = products(0, j)
-            early = sb(f"y_early{j}", [P, 2, P], F32)
-            if j == 1:
-                rounded(nc.scalar.copy, 0, j, held)
-            nc.scalar.copy(early[:].rearrange("p r q -> p (r q)"), held)
-            nc.sync.dma_start(out_rows[:, 0:2, j * P : (j + 1) * P], early[:])
-            if j == 0:
-                rounded(nc.vector.tensor_copy, 0, j, held)
+        def copied(copy, name, n, j, held, at):
+            plain = sb(name, [P, 2, P], F32, at=at)
+            copy(plain[:].rearrange("p r q -> p (r q)"), held)
+            return plain
+
+        early = [products(0, j) for j in range(HALVES)]
+        plain = copied(nc.scalar.copy, "y_early0", 0, 0, early[0], RECIP + 2 * I)
+        nc.sync.dma_start(out_rows[:, 0:2, 0:P], plain[:])
+        rounded(nc.vector.tensor_copy, 0, 0, early[0])
+        rounded(nc.scalar.copy, 0, 1, early[1])
+        late = [products(1, j) for j in range(HALVES)]
+        rounded(nc.vector.tensor_copy, 1, 0, late[0])
+        rounded(nc.scalar.copy, 1, 1, late[1])
+        plain = copied(nc.scalar.copy, "y_early1", 0, 1, early[1], LAST)
+        nc.sync.dma_start(out_rows[:, 0:2, P:Q], plain[:])
         y_late = sb("y_late", [P, 2, Q], F32)
         for j, copy in enumerate((nc.vector.tensor_copy, nc.scalar.copy)):
-            held = products(1, j)
-            rounded(copy, 1, j, held)
-            copy(y_late[:, :, j * P : (j + 1) * P], held.rearrange("p (r q) -> p r q", q=P))
+            copy(y_late[:, :, j * P : (j + 1) * P], late[j].rearrange("p (r q) -> p r q", q=P))
         nc.scalar.dma_start(out_rows[:, 2:PACK, :], y_late[:])
-        for j in range(HALVES):
-            cols = slice(j * P, (j + 1) * P)
-            quantise(y_codes[:, cols], y_scales[:, cols], y_grouped[j][:].rearrange("p q r -> p (q r)"))
+        quantise(y_codes[:], y_scales[:], y_grouped[:].rearrange("p q r -> p (q r)"))
         nc.sync.dma_start(out_words, y_codes[:].bitcast(I32))
         for quad in range(QUADS):
             queue = nc.sync if quad < 2 else nc.scalar

@@ -28,8 +28,7 @@ KN_ROW = QUERIES
 KN_LISTED = QUERIES - 8 * I
 ROOTS = QUERIES - 24 * I
 CODES = QUERIES - 12 * I
-RECIP = QUERIES - 32 * I
-LAST = QUERIES - 36 * I
+RECIP = QUERIES - 40 * I
 SHARE = 256
 
 
@@ -252,7 +251,7 @@ def tile_attend_necread_pl_kernel(
         grouped3 = group_values(2, 1, nc.scalar.copy, None)
         wq.append(quantise_weights(1, w_grouped[1]))
         quantise_values(1, grouped2, None)
-        quantise_values(2, grouped3, LAST)
+        quantise_values(2, grouped3, None)
 
         out_rows = out_0.rearrange("(p r) q -> p r q", r=PACK)
         out_words = out_1[0].rearrange("p q r -> p (q r)").bitcast(I32)
@@ -270,38 +269,33 @@ def tile_attend_necread_pl_kernel(
 
         y_scales = sb("y_scales", [P, Q], U8)
         y_codes = sb("y_codes", [P, Q], U32)
-        y_grouped = sb("y_grouped", [P, Q, PACK], BF16, at=RECIP + 4 * I)
+        y_grouped = sb("y_grouped", [P, Q, PACK], BF16)
+        y_plain = sb("y_plain", [P, PACK, Q], F32, at=RECIP + 4 * I)
         pair_banks = ((5, 6), (2, 0))
 
-        def products(n, j):
-            pair_ps = bank(f"y_ps{n}{j}", pair_banks[n][j])
+        def products(n, j, copy):
+            held = bank(f"y_ps{n}{j}", pair_banks[n][j])
             for m in range(2):
-                product(2 * n + m, j, pair_ps[:, m * P : (m + 1) * P])
-            return pair_ps[:, 0 : 2 * P]
+                product(2 * n + m, j, held[:, m * P : (m + 1) * P])
+            copy(
+                y_plain[:, 2 * n : 2 * n + 2, j * P : (j + 1) * P],
+                held[:, 0 : 2 * P].rearrange("p (r q) -> p r q", q=P),
+            )
 
-        def rounded(copy, n, j, held):
-            copy(y_grouped[:, j * P : (j + 1) * P, 2 * n : 2 * n + 2], held.rearrange("p (r q) -> p q r", q=P))
-
-        def copied(copy, name, n, j, held, at):
-            plain = sb(name, [P, 2, P], F32, at=at)
-            copy(plain[:].rearrange("p r q -> p (r q)"), held)
-            return plain
-
-        early = [products(0, j) for j in range(HALVES)]
-        plain = copied(nc.scalar.copy, "y_early0", 0, 0, early[0], RECIP + 2 * I)
-        nc.sync.dma_start(out_rows[:, 0:2, 0:P], plain[:])
-        rounded(nc.vector.tensor_copy, 0, 0, early[0])
-        rounded(nc.scalar.copy, 0, 1, early[1])
-        late = [products(1, j) for j in range(HALVES)]
-        rounded(nc.vector.tensor_copy, 1, 0, late[0])
-        rounded(nc.scalar.copy, 1, 1, late[1])
-        plain = copied(nc.scalar.copy, "y_early1", 0, 1, early[1], LAST)
-        nc.sync.dma_start(out_rows[:, 0:2, P:Q], plain[:])
-        y_late = sb("y_late", [P, 2, Q], F32)
-        for j, copy in enumerate((nc.vector.tensor_copy, nc.scalar.copy)):
-            copy(y_late[:, :, j * P : (j + 1) * P], late[j].rearrange("p (r q) -> p r q", q=P))
-        nc.scalar.dma_start(out_rows[:, 2:PACK, :], y_late[:])
-        quantise(y_codes[:], y_scales[:], y_grouped[:].rearrange("p q r -> p (q r)"))
+        for j in range(HALVES):
+            products(0, j, nc.scalar.copy)
+        nc.sync.dma_start(out_rows[:, 0:2, :], y_plain[:, 0:2, :])
+        products(1, 0, nc.vector.tensor_copy)
+        products(1, 1, nc.scalar.copy)
+        nc.sync.dma_start(out_rows[:, 2:PACK, :], y_plain[:, 2:PACK, :])
+        for copy, a, b in ((nc.vector.tensor_copy, 0, P), (nc.scalar.copy, Q - P // 2, Q), (nc.vector.tensor_copy, P, Q - P // 2)):
+            copy(
+                y_grouped[:, a:b, :].rearrange("p (c i) r -> p c r i", i=4),
+                y_plain[:, :, a:b].rearrange("p r (c i) -> p c r i", i=4),
+            )
+        for j in range(HALVES):
+            cols = slice(j * P, (j + 1) * P)
+            quantise(y_codes[:, cols], y_scales[:, cols], y_grouped[:, cols, :].rearrange("p q r -> p (q r)"))
         nc.sync.dma_start(out_words, y_codes[:].bitcast(I32))
         for quad in range(QUADS):
             queue = nc.sync if quad < 2 else nc.scalar

@@ -28,7 +28,7 @@ KN_ROW = QUERIES
 KN_LISTED = QUERIES - 8 * I
 ROOTS = QUERIES - 24 * I
 CODES = QUERIES - 12 * I
-RECIP = QUERIES - 40 * I
+RECIP = QUERIES - 42 * I
 SHARE = 256
 
 
@@ -205,7 +205,7 @@ def tile_attend_necread_pl_kernel(
 
 
         def weights(j, recip, inv):
-            w = sb(f"w{j}", [P, I], BF16, at=val_at[1] + 12 * I if j == 0 else None)
+            w = sb(f"w{j}", [P, I], BF16)
             nc.vector.scalar_tensor_tensor(w[:], recip[:], inv, size_ps[:], ALU.mult, ALU.mult)
             words = w[:].bitcast(F32)
             w_ps = bank(f"w_ps{j}", 4 - 3 * j)
@@ -229,21 +229,20 @@ def tile_attend_necread_pl_kernel(
         totals = sb("totals", [P, HALVES], F32)
         recip0 = reciprocals(0, RECIP)
         recip1 = reciprocals(1, None)
-        inv0 = sb("inv0", [P, 1], F32)
-        nc.vector.reciprocal(inv0[:], totals[:, 0:1])
+        inv = sb("inv", [P, HALVES], F32)
+        for j in range(HALVES):
+            nc.vector.reciprocal(inv[:, j : j + 1], totals[:, j : j + 1])
         picked1 = sb("val_picked1", [P, I], BF16, at=ROOTS)
-        gather_values(1, 320, picked1[:])
-        inv1 = sb("inv1", [P, 1], F32, at=val_at[1])
-        nc.vector.reciprocal(inv1[:], totals[:, 1:2])
+        gather_values(1, I, picked1[:])
         picked2 = sb("val_picked2", [P, I], BF16, at=ROOTS + 4 * I)
         gather_values(2, I, picked2[:])
-        w_ps0 = weights(0, recip0, inv0[:])
-        w_ps1 = weights(1, recip1, inv1[:])
-        grouped01 = group_values(0, 2, nc.scalar.copy, val_at[2] + 8 * I)
+        w_ps0 = weights(0, recip0, inv[:, 0:1])
+        w_ps1 = weights(1, recip1, inv[:, 1:2])
         w_grouped = [sb(f"w_grouped{j}", [P, I], BF16, at=val_at[3] if j == 1 else None)[:] for j in range(HALVES)]
         group_weights(w_ps0, w_grouped[0], nc.vector.tensor_copy)
+        grouped01 = group_values(0, 2, nc.vector.tensor_copy, RECIP - 2 * I)
         picked3 = sb("val_picked3", [P, I], BF16, at=RECIP + 3 * I)
-        gather_values(3, 288, picked3[:])
+        gather_values(3, SHARE, picked3[:])
         quantise_values(0, grouped01, val_at[3] + 6 * I)
         wq = [quantise_weights(0, w_grouped[0])]
         group_weights(w_ps1, w_grouped[1], nc.scalar.copy)
@@ -271,22 +270,23 @@ def tile_attend_necread_pl_kernel(
         y_codes = sb("y_codes", [P, Q], U32)
         y_grouped = sb("y_grouped", [P, Q, PACK], BF16)
         y_plain = sb("y_plain", [P, PACK, Q], F32, at=RECIP + 4 * I)
-        pair_banks = ((5, 6), (2, 0))
 
-        def products(n, j, copy):
-            held = bank(f"y_ps{n}{j}", pair_banks[n][j])
-            for m in range(2):
-                product(2 * n + m, j, held[:, m * P : (m + 1) * P])
+        def products(planes, j, number, copy):
+            held = bank(f"y_ps{planes.start}{j}", number)
+            for m, r in enumerate(planes):
+                product(r, j, held[:, m * P : (m + 1) * P])
             copy(
-                y_plain[:, 2 * n : 2 * n + 2, j * P : (j + 1) * P],
-                held[:, 0 : 2 * P].rearrange("p (r q) -> p r q", q=P),
+                y_plain[:, planes.start : planes.stop, j * P : (j + 1) * P],
+                held[:, 0 : len(planes) * P].rearrange("p (r q) -> p r q", q=P),
             )
 
         for j in range(HALVES):
-            products(0, j, nc.scalar.copy)
+            products(range(0, 2), j, 5 + j, nc.scalar.copy)
         nc.sync.dma_start(out_rows[:, 0:2, :], y_plain[:, 0:2, :])
-        products(1, 0, nc.vector.tensor_copy)
-        products(1, 1, nc.scalar.copy)
+        for j in range(HALVES):
+            products(range(2, 3), j, 4 - 3 * j, nc.vector.tensor_copy)
+        products(range(3, 4), 0, 2, nc.vector.tensor_copy)
+        products(range(3, 4), 1, 0, nc.scalar.copy)
         nc.sync.dma_start(out_rows[:, 2:PACK, :], y_plain[:, 2:PACK, :])
         for copy, a, b in ((nc.vector.tensor_copy, 0, P), (nc.scalar.copy, Q - P // 2, Q), (nc.vector.tensor_copy, P, Q - P // 2)):
             copy(

@@ -49,6 +49,10 @@ def tile_attend_necread_pl_kernel(
         def quantise(codes, scales, grouped):
             nc.vector.quantize_mx(out=codes.bitcast(FP8X4), scales=scales, in_=grouped)
 
+        key_word_win = sb("key_word_win", [P, T], U16)
+        nc.sync.dma_start(key_word_win[:].bitcast(I32), keys_words[0].bitcast(I32))
+        kn_win = sb("kn_win", [P, T], F32)
+        nc.sync.dma_start(kn_win[P - 1 : P, :], kn[0:1, :])
         offsets = keep.tile([P, I // 16], U16, name="offsets")
         nc.sync.dma_start(offsets[:], offs)
 
@@ -58,21 +62,16 @@ def tile_attend_necread_pl_kernel(
         ident = sb("ident", [P, P], F32)
         spans = ((0, 48, LANDING - 128), (48, 80, val_at[1]), (80, 104, val_at[2] + 1024), (104, 128, val_at[3]))
         zeros = [sb(f"zeros{a}", [P, b - a], F32, at=at) for a, b, at in spans]
-        for source in zeros:
-            nc.gpsimd.memset(source[:], 0.0)
         for (a, b, at), source in zip(spans, zeros):
+            nc.gpsimd.memset(source[:], 0.0)
             nc.gpsimd.affine_select(
                 out=ident[:, a:b], in_=source[:], compare_op=ALU.not_equal, fill=1.0,
                 base=-a, pattern=[[-1, b - a]], channel_multiplier=1,
             )
         warm = sb("warm", [P, 1], F32)
         nc.vector.memset(warm[:], 1.0)
-        kn_win = sb("kn_win", [P, T], F32)
         nc.vector.memset(kn_win[0 : P - 1, :].bitcast(I32), 0)
 
-        nc.sync.dma_start(kn_win[P - 1 : P, :], kn[0:1, :])
-        key_word_win = sb("key_word_win", [P, T], U16)
-        nc.sync.dma_start(key_word_win[:].bitcast(I32), keys_words[0].bitcast(I32))
         q_raw = sb("q_raw", [P, PACK, Q], F32, at=QUERIES)
         nc.sync.dma_start(q_raw[:], query.rearrange("(p j) q -> p j q", j=PACK))
         for quad in range(QUADS):
@@ -146,8 +145,9 @@ def tile_attend_necread_pl_kernel(
 
         dists = []
         for j in range(HALVES):
-            score_ps = bank(f"score_ps{j}", j)
+            dist = sb(f"dist{j}", [P, I], F32)
             for slots in (slice(0, SHARE), slice(SHARE, I)) if j == 0 else (slice(0, I),):
+                score_ps = bank(f"score_ps{j}{slots.start}", 4 if slots.start else j)
                 nc.tensor.matmul_mx(
                     out=score_ps[:, slots],
                     lhsT=q_codes[:, j * P : (j + 1) * P].bitcast(FP8X4),
@@ -157,8 +157,7 @@ def tile_attend_necread_pl_kernel(
                     start=True,
                     stop=True,
                 )
-            dist = sb(f"dist{j}", [P, I], F32)
-            nc.vector.scalar_tensor_tensor(dist[:], score_ps[:], -2.0, kn_row[:], ALU.mult, ALU.add)
+                nc.vector.scalar_tensor_tensor(dist[:, slots], score_ps[:, slots], -2.0, kn_row[:, slots], ALU.mult, ALU.add)
             dists.append(dist[:].rearrange("p (s u e) -> p u s e", u=2, e=2))
 
         roots, mags, signs = [], [], []

@@ -30,6 +30,7 @@ ROOTS = QUERIES - 24 * I
 CODES = QUERIES - 12 * I
 RECIP = QUERIES - 42 * I
 SHARE = 256
+KN_SHARE = 128
 
 
 def tile_attend_necread_pl_kernel(
@@ -97,40 +98,47 @@ def tile_attend_necread_pl_kernel(
         nc.scalar.activation(warm_out[:], warm[:], ACT.Abs_reciprocal_sqrt)
 
         kn_g = sb("kn_g", [P, I], F32, at=KN_LISTED)
-        nc.vector.tensor_copy(kn_g[:, 0:SHARE], kn_win[:].indirect(offsets[:, 0 : SHARE // 16]))
-        nc.scalar.activation(kn_g[:, SHARE:I], kn_win[:].indirect(offsets[:, SHARE // 16 : I // 16]), ACT.Copy)
+        nc.vector.tensor_copy(kn_g[:, 0:KN_SHARE], kn_win[:].indirect(offsets[:, 0 : KN_SHARE // 16]))
+        for a, b in ((KN_SHARE, SHARE), (SHARE, I)):
+            nc.scalar.activation(kn_g[:, a:b], kn_win[:].indirect(offsets[:, a // 16 : b // 16]), ACT.Copy)
         key_words = sb("key_words", [P, I], U16)
         nc.vector.tensor_copy(key_words[:], key_word_win[:].indirect(offsets[:]))
         key_scales = sb("key_scales", [P, I], U8)
 
-        kn_ps = bank("kn_ps", 2)
-        for c in range(4):
-            nc.tensor.transpose(kn_ps[:, c * P : (c + 1) * P], kn_g[:, c * P : (c + 1) * P], ident[:])
         kn_col = picked0[:].bitcast(F32)[:, 0:4]
-        nc.scalar.copy(kn_col, kn_ps[:, P - 1 : BANK : P])
+        for n in range(2):
+            kn_ps = bank(f"kn_ps{n}", 6 + n)
+            for c in range(2):
+                nc.tensor.transpose(kn_ps[:, c * P : (c + 1) * P], kn_g[:, (2 * n + c) * P : (2 * n + c + 1) * P], ident[:])
+            nc.scalar.copy(kn_col[:, 2 * n : 2 * n + 2], kn_ps[:, P - 1 : 2 * P : P])
 
-        q_codes = sb("q_codes", [P, Q], U32, at=CODES)
-        q_scales = []
-        for j in range(HALVES):
-            nc.vector.tensor_copy(
-                key_scales[:, j * SHARE : (j + 1) * SHARE],
-                key_scale_win[:].indirect(offsets[:, j * SHARE // 16 : (j + 1) * SHARE // 16]),
-            )
-            q_scales.append(sb(f"q_scales{j}", [P, P], U8, "key_scale_win" if j == 1 else None))
-            q_grouped = sb(f"q_grouped{j}", [P, P, PACK], BF16, at=KN_LISTED + 2 * I * j)
-            nc.scalar.copy(
-                q_grouped[:].rearrange("p (c i) j -> p c j i", i=4),
+        pieces = (slice(0, SHARE), slice(SHARE, I))
+        q_grouped = []
+        for j, copy in enumerate((nc.vector.tensor_copy, nc.scalar.copy)):
+            q_grouped.append(sb(f"q_grouped{j}", [P, P, PACK], BF16))
+            copy(
+                q_grouped[j][:].rearrange("p (c i) j -> p c j i", i=4),
                 q_raw[:, :, j * P : (j + 1) * P].rearrange("p j (c i) -> p c j i", i=4),
             )
-            quantise(q_codes[:, j * P : (j + 1) * P], q_scales[j][:], q_grouped[:].rearrange("p q j -> p (q j)"))
+        q_codes = sb("q_codes", [P, Q], U32, at=CODES)
+        q_scales = [sb(f"q_scales{j}", [P, P], U8) for j in range(HALVES)]
 
-        kn_row_ps = bank("kn_row_ps", 3)
-        for c in range(4):
-            nc.tensor.transpose(
-                kn_row_ps[:, c * P : (c + 1) * P], kn_col[:, c : c + 1].to_broadcast([P, P]), ident[:]
-            )
+        def gather_scales(s):
+            nc.vector.tensor_copy(key_scales[:, s], key_scale_win[:].indirect(offsets[:, s.start // 16 : s.stop // 16]))
+
+        gather_scales(pieces[0])
+        for j in range(HALVES):
+            quantise(q_codes[:, j * P : (j + 1) * P], q_scales[j][:], q_grouped[j][:].rearrange("p q j -> p (q j)"))
+        gather_scales(pieces[1])
+
         kn_row = sb("kn_row", [P, I], F32, at=KN_ROW)
-        nc.scalar.activation(kn_row[:], kn_row_ps[:], ACT.Copy, bias=0.1)
+        for n, s in enumerate(pieces):
+            kn_row_ps = bank(f"kn_row_ps{n}", 2 + n)
+            for c in range(2):
+                nc.tensor.transpose(
+                    kn_row_ps[:, c * P : (c + 1) * P], kn_col[:, 2 * n + c : 2 * n + c + 1].to_broadcast([P, P]), ident[:]
+                )
+            nc.scalar.activation(kn_row[:, s], kn_row_ps[:, 0 : 2 * P], ACT.Copy, bias=0.1)
 
         val_ps = [bank("val_ps01", 2), bank("val_ps2", 3), bank("val_ps3", 7)]
 
@@ -143,11 +151,11 @@ def tile_attend_necread_pl_kernel(
             for u in range(2):
                 nc.tensor.transpose(val_ps[n][:, first + u * P : first + (u + 1) * P], words[:, u : 2 * P : 2], ident[:])
 
-        dists = []
-        for j in range(HALVES):
-            dist = sb(f"dist{j}", [P, I], F32)
-            for slots in (slice(0, SHARE), slice(SHARE, I)) if j == 0 else (slice(0, I),):
-                score_ps = bank(f"score_ps{j}{slots.start}", 4 if slots.start else j)
+        dist_tiles = [sb(f"dist{j}", [P, I], F32) for j in range(HALVES)]
+        dists = [dist[:].rearrange("p (s u e) -> p u s e", u=2, e=2) for dist in dist_tiles]
+        for n, slots in enumerate(pieces):
+            for j, dist in enumerate(dist_tiles):
+                score_ps = bank(f"score_ps{j}{n}", ((1, 4), (5, 0))[j][n])
                 nc.tensor.matmul_mx(
                     out=score_ps[:, slots],
                     lhsT=q_codes[:, j * P : (j + 1) * P].bitcast(FP8X4),
@@ -158,7 +166,6 @@ def tile_attend_necread_pl_kernel(
                     stop=True,
                 )
                 nc.vector.scalar_tensor_tensor(dist[:, slots], score_ps[:, slots], -2.0, kn_row[:, slots], ALU.mult, ALU.add)
-            dists.append(dist[:].rearrange("p (s u e) -> p u s e", u=2, e=2))
 
         roots, mags, signs = [], [], []
         for j in range(HALVES):

from contextlib import ExitStack

import concourse.mybir as mybir

D, T, I, Q, E = 512, 2048, 512, 256, 512
FLOPS = 2 * D * Q * I + 2 * I * E * Q

F32 = mybir.dt.float32
BF16 = mybir.dt.bfloat16
I32 = mybir.dt.int32
U32 = mybir.dt.uint32
U16 = mybir.dt.uint16
U8 = mybir.dt.uint8
FP8X4 = mybir.dt.float8_e4m3fn_x4
FP4X4 = mybir.dt.float4_e2m1fn_x4
ACT = mybir.ActivationFunctionType
ALU = mybir.AluOpType

P = 128
PACK = 4
BANK = 512
HALVES = Q // P
QUADS = 4
LANDING = 160 * 1024
WINDOW = 4 * T
QUERIES = LANDING - WINDOW
KN_ROW = QUERIES
KN_LISTED = QUERIES - 8 * I
ROOTS = QUERIES - 24 * I
CODES = QUERIES - 12 * I
RECIP = QUERIES - 42 * I
SHARE = 256
KN_SHARE = 128


def tile_attend_necread_pl_kernel(
    tc, query, keys_words, keys_scales, kn, qn, size, vals, offs, out_0, out_1, out_2
):
    nc = tc.nc
    with ExitStack() as ctx:
        keep = ctx.enter_context(tc.tile_pool(name="keep", bufs=1))
        psum = ctx.enter_context(tc.psum_pool(name="psum", bufs=1))

        def sb(name, shape, dtype, place=None, at=None):
            return keep.tile(shape, dtype, name=name, tag=place or name, align_bytes=64, offset=at)

        def bank(name, number):
            return psum.tile([P, BANK], F32, name=name, tag=f"bank{number}")

        def quantise(codes, scales, grouped):
            nc.vector.quantize_mx(out=codes.bitcast(FP8X4), scales=scales, in_=grouped)

        key_word_win = sb("key_word_win", [P, T], U16)
        nc.sync.dma_start(key_word_win[:].bitcast(I32), keys_words[0].bitcast(I32))
        kn_win = sb("kn_win", [P, T], F32)
        nc.sync.dma_start(kn_win[P - 1 : P, :], kn[0:1, :])
        offsets = keep.tile([P, I // 16], U16, name="offsets")
        nc.sync.dma_start(offsets[:], offs)

        val_at = [LANDING + (WINDOW + 128) * r for r in range(PACK)]
        key_scale_win = sb("key_scale_win", [P, T], U8)
        nc.gpsimd.memset(key_scale_win[:].bitcast(U32), 0)
        ident = sb("ident", [P, P], F32)
        spans = ((0, 48, LANDING - 128), (48, 80, val_at[1]), (80, 104, val_at[2] + 1024), (104, 128, val_at[3]))
        zeros = [sb(f"zeros{a}", [P, b - a], F32, at=at) for a, b, at in spans]
        for (a, b, at), source in zip(spans, zeros):
            nc.gpsimd.memset(source[:], 0.0)
            nc.gpsimd.affine_select(
                out=ident[:, a:b], in_=source[:], compare_op=ALU.not_equal, fill=1.0,
                base=-a, pattern=[[-1, b - a]], channel_multiplier=1,
            )
        warm = sb("warm", [P, 1], F32)
        nc.vector.memset(warm[:], 1.0)
        nc.vector.memset(kn_win[0 : P - 1, :].bitcast(I32), 0)

        q_raw = sb("q_raw", [P, PACK, Q], F32, at=QUERIES)
        nc.sync.dma_start(q_raw[:], query.rearrange("(p j) q -> p j q", j=PACK))
        for quad in range(QUADS):
            nc.sync.dma_start(
                key_scale_win[quad:P:32, :].bitcast(I32),
                keys_scales[0, quad:16:4, :].bitcast(I32),
            )
        picked0 = sb("val_picked0", [P, I + 32], BF16, at=LANDING - 128 - 2 * I)
        qn_col = picked0[:].bitcast(F32)[:, I // 2 - 1 : I // 2 + 1]
        vals_rows = vals.rearrange("(p r) t -> r p t", r=PACK)
        val_wins = []
        for r in range(PACK):
            win = sb(f"val_win{r}", [P, T], F32, at=val_at[r])
            nc.sync.dma_start(win[:], vals_rows[r])
            val_wins.append(win)
            if r == 0:
                with nc.allow_non_contiguous_dma(reason="one number a query row"):
                    nc.sync.dma_start(qn_col, qn.rearrange("(j p) o -> p (j o)", p=P))
                size_col = sb("size_col", [P, PACK], F32, at=LANDING - 64)
                nc.sync.dma_start(size_col[:], size.rearrange("o (p t) -> p (o t)", t=PACK))

        warm_out = sb("warm_out", [P, 1], F32)
        nc.scalar.activation(warm_out[:], warm[:], ACT.Abs_reciprocal_sqrt)

        kn_g = sb("kn_g", [P, I], F32, at=KN_LISTED)
        nc.vector.tensor_copy(kn_g[:, 0:KN_SHARE], kn_win[:].indirect(offsets[:, 0 : KN_SHARE // 16]))
        for a, b in ((KN_SHARE, SHARE), (SHARE, I)):
            nc.scalar.activation(kn_g[:, a:b], kn_win[:].indirect(offsets[:, a // 16 : b // 16]), ACT.Copy)
        key_words = sb("key_words", [P, I], U16)
        nc.vector.tensor_copy(key_words[:], key_word_win[:].indirect(offsets[:]))
        key_scales = sb("key_scales", [P, I], U8)

        kn_col = picked0[:].bitcast(F32)[:, 0:4]
        for n in range(2):
            kn_ps = bank(f"kn_ps{n}", 6 + n)
            for c in range(2):
                nc.tensor.transpose(kn_ps[:, c * P : (c + 1) * P], kn_g[:, (2 * n + c) * P : (2 * n + c + 1) * P], ident[:])
            nc.scalar.copy(kn_col[:, 2 * n : 2 * n + 2], kn_ps[:, P - 1 : 2 * P : P])

        pieces = (slice(0, SHARE), slice(SHARE, I))
        q_grouped = []
        for j, copy in enumerate((nc.vector.tensor_copy, nc.scalar.copy)):
            q_grouped.append(sb(f"q_grouped{j}", [P, P, PACK], BF16))
            copy(
                q_grouped[j][:].rearrange("p (c i) j -> p c j i", i=4),
                q_raw[:, :, j * P : (j + 1) * P].rearrange("p j (c i) -> p c j i", i=4),
            )
        q_codes = sb("q_codes", [P, Q], U32, at=CODES)
        q_scales = [sb(f"q_scales{j}", [P, P], U8) for j in range(HALVES)]

        def gather_scales(s):
            nc.vector.tensor_copy(key_scales[:, s], key_scale_win[:].indirect(offsets[:, s.start // 16 : s.stop // 16]))

        gather_scales(pieces[0])
        for j in range(HALVES):
            quantise(q_codes[:, j * P : (j + 1) * P], q_scales[j][:], q_grouped[j][:].rearrange("p q j -> p (q j)"))
        gather_scales(pieces[1])

        kn_row = sb("kn_row", [P, I], F32, at=KN_ROW)
        for n, s in enumerate(pieces):
            kn_row_ps = bank(f"kn_row_ps{n}", 2 + n)
            for c in range(2):
                nc.tensor.transpose(
                    kn_row_ps[:, c * P : (c + 1) * P], kn_col[:, 2 * n + c : 2 * n + c + 1].to_broadcast([P, P]), ident[:]
                )
            nc.scalar.activation(kn_row[:, s], kn_row_ps[:, 0 : 2 * P], ACT.Copy, bias=0.1)

        val_ps = [bank("val_ps01", 2), bank("val_ps2", 3), bank("val_ps3", 7)]

        def gather_values(r, share, picked):
            nc.scalar.activation(picked[:, 0:share], val_wins[r][:].indirect(offsets[:, 0 : share // 16]), ACT.Copy)
            if share < I:
                nc.vector.tensor_copy(picked[:, share:I], val_wins[r][:].indirect(offsets[:, share // 16 : I // 16]))
            words = picked.bitcast(F32)
            n, first = max(r - 1, 0), (r == 1) * 2 * P
            for u in range(2):
                nc.tensor.transpose(val_ps[n][:, first + u * P : first + (u + 1) * P], words[:, u : 2 * P : 2], ident[:])

        dist_tiles = [sb(f"dist{j}", [P, I], F32) for j in range(HALVES)]
        dists = [dist[:].rearrange("p (s u e) -> p u s e", u=2, e=2) for dist in dist_tiles]
        for n, slots in enumerate(pieces):
            for j, dist in enumerate(dist_tiles):
                score_ps = bank(f"score_ps{j}{n}", ((1, 4), (5, 0))[j][n])
                nc.tensor.matmul_mx(
                    out=score_ps[:, slots],
                    lhsT=q_codes[:, j * P : (j + 1) * P].bitcast(FP8X4),
                    lhsT_scale=q_scales[j][:],
                    rhs=key_words[:, slots].bitcast(FP4X4),
                    rhs_scale=key_scales[:, slots],
                    start=True,
                    stop=True,
                )
                nc.vector.scalar_tensor_tensor(dist[:, slots], score_ps[:, slots], -2.0, kn_row[:, slots], ALU.mult, ALU.add)

        roots, mags, signs = [], [], []
        for j in range(HALVES):
            above = sb(f"above{j}", [P, 2, P, 2], BF16, at=CODES if j == 0 else None)
            nc.vector.tensor_scalar(above[:], dists[j], qn_col[:, j : j + 1], 0.0, ALU.add, ALU.is_ge)
            signs.append(above[:].rearrange("p u s e -> p (u s e)"))
            root = sb(f"root{j}", [P, 2, P, 2], F32, at=ROOTS + 4 * I * j)
            nc.scalar.activation(root[:], dists[j], ACT.Abs_reciprocal_sqrt, bias=qn_col[:, j : j + 1])
            roots.append(root)
        for j in range(HALVES):
            mag = sb(f"mag{j}", [P, 2, P, 2], F32)
            nc.scalar.activation(mag[:], roots[j][:], ACT.Square)
            mags.append(mag[:].rearrange("p u s e -> p (u s e)"))

        size_ps = bank("size_ps", 0)
        size_dealt = size_ps[:].rearrange("p (u s e) -> p u e s", u=2, e=2)
        for t in range(PACK):
            nc.tensor.transpose(
                size_dealt[:, t // 2, t % 2, :], size_col[:, t : t + 1].to_broadcast([P, P]), ident[:]
            )

        vq = []

        def group_values(n, planes, copy, at):
            grouped = sb(f"val_grouped{n}", [P, planes * I], BF16, at=at)
            copy(
                grouped[:].bitcast(F32).rearrange("p (r c u) -> p r c u", c=P, u=2),
                val_ps[n][:, 0 : planes * 2 * P].rearrange("p (r u c) -> p r c u", c=P, u=2),
            )
            return grouped

        def quantise_values(n, grouped, at):
            width = grouped.shape[1] // PACK
            codes = sb(f"val_codes{n}", [P, width], U32, at=at)
            scales = sb(f"val_scales{n}", [P, width], U8)
            quantise(codes[:], scales[:], grouped[:])
            vq.extend((codes[:, m : m + P], scales[:, m : m + P]) for m in range(0, width, P))

        def reciprocals(j, at):
            recip = sb(f"recip{j}", [P, I], F32, at=at)
            nc.vector.scalar_tensor_tensor(recip[:], signs[j], -0.5, mags[j], ALU.add, ALU.mult, accum_out=totals[:, j : j + 1])
            return recip


        def weights(j, recip, inv):
            w = sb(f"w{j}", [P, I], BF16)
            nc.vector.scalar_tensor_tensor(w[:], recip[:], inv, size_ps[:], ALU.mult, ALU.mult)
            words = w[:].bitcast(F32)
            w_ps = bank(f"w_ps{j}", 4 - 3 * j)
            for u in range(2):
                nc.tensor.transpose(w_ps[:, u * P : (u + 1) * P], words[:, u * P : (u + 1) * P], ident[:])
            return w_ps

        def group_weights(w_ps, grouped, copy):
            copy(
                grouped.bitcast(F32).rearrange("p (c u) -> p c u", u=2),
                w_ps[:, 0 : 2 * P].rearrange("p (u c) -> p c u", u=2),
            )

        def quantise_weights(j, grouped):
            codes = sb(f"w_codes{j}", [P, P], U32, at=val_at[3] + 4 * I if j == 0 else None)
            scales = sb(f"w_scales{j}", [P, P], U8)
            quantise(codes[:], scales[:], grouped)
            return codes, scales

        gather_values(0, SHARE, picked0[:, 0:I])
        totals = sb("totals", [P, HALVES], F32)
        recip0 = reciprocals(0, RECIP)
        recip1 = reciprocals(1, None)
        inv = sb("inv", [P, HALVES], F32)
        for j in range(HALVES):
            nc.vector.reciprocal(inv[:, j : j + 1], totals[:, j : j + 1])
        picked1 = sb("val_picked1", [P, I], BF16, at=ROOTS)
        gather_values(1, I, picked1[:])
        picked2 = sb("val_picked2", [P, I], BF16, at=ROOTS + 4 * I)
        gather_values(2, I, picked2[:])
        w_ps0 = weights(0, recip0, inv[:, 0:1])
        w_ps1 = weights(1, recip1, inv[:, 1:2])
        w_grouped = [sb(f"w_grouped{j}", [P, I], BF16, at=val_at[3] if j == 1 else None)[:] for j in range(HALVES)]
        group_weights(w_ps0, w_grouped[0], nc.vector.tensor_copy)
        grouped01 = group_values(0, 2, nc.vector.tensor_copy, RECIP - 2 * I)
        picked3 = sb("val_picked3", [P, I], BF16, at=RECIP + 3 * I)
        gather_values(3, SHARE, picked3[:])
        quantise_values(0, grouped01, val_at[3] + 6 * I)
        wq = [quantise_weights(0, w_grouped[0])]
        group_weights(w_ps1, w_grouped[1], nc.scalar.copy)
        grouped2 = group_values(1, 1, nc.scalar.copy, val_at[3] + 2 * I)
        grouped3 = group_values(2, 1, nc.scalar.copy, None)
        wq.append(quantise_weights(1, w_grouped[1]))
        quantise_values(1, grouped2, None)
        quantise_values(2, grouped3, None)

        out_rows = out_0.rearrange("(p r) q -> p r q", r=PACK)
        out_words = out_1[0].rearrange("p q r -> p (q r)").bitcast(I32)

        def product(r, j, out):
            nc.tensor.matmul_mx(
                out=out,
                lhsT=vq[r][0].bitcast(FP8X4),
                lhsT_scale=vq[r][1],
                rhs=wq[j][0][:].bitcast(FP8X4),
                rhs_scale=wq[j][1][:],
                start=True,
                stop=True,
            )

        y_scales = sb("y_scales", [P, Q], U8)
        y_codes = sb("y_codes", [P, Q], U32)
        y_grouped = sb("y_grouped", [P, Q, PACK], BF16)
        y_plain = sb("y_plain", [P, PACK, Q], F32, at=RECIP + 4 * I)

        def products(planes, j, number, copy):
            held = bank(f"y_ps{planes.start}{j}", number)
            for m, r in enumerate(planes):
                product(r, j, held[:, m * P : (m + 1) * P])
            copy(
                y_plain[:, planes.start : planes.stop, j * P : (j + 1) * P],
                held[:, 0 : len(planes) * P].rearrange("p (r q) -> p r q", q=P),
            )

        for j in range(HALVES):
            products(range(0, 2), j, 5 + j, nc.scalar.copy)
        nc.sync.dma_start(out_rows[:, 0:2, :], y_plain[:, 0:2, :])
        for j in range(HALVES):
            products(range(2, 3), j, 4 - 3 * j, nc.vector.tensor_copy)
        products(range(3, 4), 0, 2, nc.vector.tensor_copy)
        products(range(3, 4), 1, 0, nc.scalar.copy)
        nc.sync.dma_start(out_rows[:, 2:PACK, :], y_plain[:, 2:PACK, :])
        for copy, a, b in ((nc.vector.tensor_copy, 0, P), (nc.scalar.copy, Q - P // 2, Q), (nc.vector.tensor_copy, P, Q - P // 2)):
            copy(
                y_grouped[:, a:b, :].rearrange("p (c i) r -> p c r i", i=4),
                y_plain[:, :, a:b].rearrange("p r (c i) -> p c r i", i=4),
            )
        for j in range(HALVES):
            cols = slice(j * P, (j + 1) * P)
            quantise(y_codes[:, cols], y_scales[:, cols], y_grouped[:, cols, :].rearrange("p q r -> p (q r)"))
        nc.sync.dma_start(out_words, y_codes[:].bitcast(I32))
        for quad in range(QUADS):
            queue = nc.sync if quad < 2 else nc.scalar
            queue.dma_start(
                out_2[0, 4 * quad : 4 * quad + 4, :].bitcast(I32),
                y_scales[32 * quad : 32 * quad + 4, :].bitcast(I32),
            )
